import numpy as np, ml_dtypes
CORES = [242,247,114,119]
N = 4
BF = ml_dtypes.bfloat16
P, TW, M, RO = 2048, 2048, 3, 5
def parts(rng):
    v = rng.integers(0, 128, (N, 8, 16, P)); v[:, :, 15] = rng.integers(0, 2, (N, 8, P))
    t = rng.integers(0, 128, (N, 8, 16, TW)); t[:, :, 15] = rng.integers(0, 2, (N, 8, TW))
    return v, t, rng.integers(1, 256, (N, 8, 16)), rng.integers(0, 2048, (N, 8, RO, M))
def pack(v, t, w, k):
    return {"x": v.reshape(N, 128, P).astype(np.float32).astype(BF), "tm": t.reshape(N, 128, TW).astype(np.float32).astype(BF),
            "wt": np.ascontiguousarray(w.reshape(N, 128, 1)).astype(np.int32),
            "km": np.repeat(k.reshape(N, 8, 1, RO * M), 16, axis=2).reshape(N, 128, RO * M).astype(np.int32)}
def aim(rng, q, noth):
    u = np.arange(1, 4096, 2); i = u.copy()
    for _ in range(4): i = (i * (2 - u * i)) & 4095
    kk = ((q - (u * u >> 5)) * i) & (P - 1)
    ok = np.flatnonzero((kk < 2048) & (((u * u >> 4) & (TW - 1)) != noth))
    s = int(rng.choice(ok)); return int(u[s]), int(kk[s])
def column(rng, w, u, s):
    c = rng.integers(0, 128, 16); c[15] = s; c[:2] = 0
    z = (u - int(np.sum(w * c))) & 4095; c[0] = z & 63; c[1] = z >> 6
    return c
def setup_inputs(rng):
    return pack(*parts(rng))
def setup_inputs_ends(rng):
    v, t, w, k = parts(rng); w[:, :, 0] = 1; w[:, :, 1] = 64; w[:, :, 15] = 0
    for r in range(N):
        o = (r + 1) % N
        for g in range(8):
            case = (g - r) % 9
            a = int(rng.integers(1, P // 4)); b = int(rng.integers(P // 2, 3 * P // 4))
            if case < 2: a, b = 0, P - 1
            if case in (2, 3): b = a + 1
            if case == 8: a, b = int(rng.integers(1, P // 8)), int(rng.integers(7 * P // 8, P - 8))
            p, q = a, b
            if case == 7 or (case < 6 and rng.random() < 0.5): p, q = b, a
            s = int(rng.integers(0, 2)); u, k[r, g, 0, 0] = aim(rng, q, -1); c = column(rng, w[r, g], u, s); h = (u * u >> 4) & (TW - 1)
            if case == 4: v[r, g, 15] = s
            v[r, g, :, p] = c; v[r, g, :, q] = c
            if case in (0, 3): v[r, g, 15, q] = 1 - s
            t[o, g, :15, h] = c[:15]
            if case == 6: v[r, g, :, int(rng.integers(a + 1, b))] = c
            if case == 7: v[r, g, :, b + 3] = c
            if case in (1, 4, 5, 7, 8):
                p2, q2 = {1: (P // 3, P // 2), 4: (a + 1, P - 1), 5: (b - 1, b + 1), 7: (a + 2, b - 2), 8: (P // 2, P - 3)}[case]
                if (case == 4 and r % 2 == 0) or rng.random() < 0.5: p2, q2 = q2, p2
                u2, k[r, g, 0, 1] = aim(rng, q2, h); c2 = column(rng, w[r, g], u2, s if case == 4 else int(rng.integers(0, 2))); h2 = (u2 * u2 >> 4) & (TW - 1)
                v[r, g, :, p2] = c2; v[r, g, :, q2] = c2; t[o, g, :15, h2] = c2[:15]; t[o, g, 0, h2] = c2[0] ^ (2 if case == 8 else 1)
            if case == 8:
                ks = np.arange(2048); zs = ((u * u >> 5) + ks * u) & (P - 1)
                ks = ks[(zs > a) & (zs < b) & (zs != P // 2)]
                k[r, g, 0, 2] = int(rng.choice(ks)); z = ((u * u >> 5) + int(k[r, g, 0, 2]) * u) & (P - 1)
                cz = c.copy(); cz[0] = c[0] ^ 1; uz = (u + int(cz[0]) - int(c[0])) & 4095
                v[r, g, :, z] = cz; t[o, g, :15, (u * uz >> 4) & (TW - 1)] = c[:15]
    return pack(v, t, w, k)
def setup_inputs_kinds(rng):
    v, t, w, k = parts(rng); w[:] = w[:1].copy(); w[:, :, 15] = 0
    for g in (0, 2, 4):
        w[:, g, 0] = 1; w[:, g, 1] = 64; w[:, g, (2 if g == 2 else 8):] = 0
        u = 3 if g == 4 else 2 * int(rng.integers(0, 2048)) + 1; c = column(rng, w[0, g], u, 0)
        if g != 2: v[:, g, :8] = c[:8, None]
        else:
            v[:, g, :2] = c[:2, None]; v[:, g, 2:15] = rng.integers(0, 41, (N, 13, P)); k[:, g, 0] = k[:, g, 0, :1].copy()
            for r in range(N): v[r, g, 2:15, ((u * u >> 5) + int(k[r, g, 0, 0]) * u) & (P - 1)] = rng.integers(120, 128, 13)
    for g in (1, 3, 5, 6, 7):
        n = 5 if g % 2 else int(rng.integers(2, 6)); kd = rng.integers(0, 128, (16, n))
        if g % 2:
            kd[:, 4] = rng.integers(40, 88, 16)
            kd[:, :4] = kd[:, 4:] + rng.integers(8, 41, (16, 4)) * (2 * rng.integers(0, 2, (16, 4)) - 1)
        for r in range(N):
            kind = rng.integers(0, n, P)
            if g % 2:
                c = r % 4; uc, u4 = [int(np.sum(w[r, g] * kd[:, i])) & 4095 for i in (c, 4)]
                kind[((u4 * u4 >> 5) + k[r, g, 0] * u4) & (P - 1)] = c
                t[(r + 1) % N, g, :15, (uc * u4 >> 4) & (TW - 1)] = (kd[:15, c] + kd[:15, 4]) >> 1
            v[r, g] = kd[:, kind]
    v[:, :, 15] = rng.integers(0, 2, (N, 8, P))
    return pack(v, t, w, k)
def setup_inputs_void(rng):
    v, t, w, k = parts(rng); w[:, :, 0] = 1; w[:, :, 1] = 64; k[:, ::2] = k[:, ::2, :1, :1].copy()
    for g in (0, 6):
        v[:, g, 2:15] &= 3; t[:, g, :15] = 124 + (t[:, g, :15] & 3)
    us = np.arange(4096); j = np.arange(P)
    for r in range(N):
        for g in range(8):
            pre = np.full(P, -1); pre[((us * us >> 5) + int(k[r, g, 0, 0]) * us) & (P - 1)] = us
            z = (pre - np.sum(w[r, g, 2:, None] * v[r, g, 2:], axis=0)) & 4095
            v[r, g, 0] = np.where(pre >= 0, z & 63, v[r, g, 0]); v[r, g, 1] = np.where(pre >= 0, z >> 6, v[r, g, 1])
            if g in (0, 6):
                u = np.sum(w[r, g, :, None] * v[r, g], axis=0) & 4095; q = ((u * u >> 5) + int(k[r, g, 0, 0]) * u) & (P - 1)
                h = (u * u[q] >> 4) & (TW - 1); free = np.flatnonzero((q == j) & ~np.isin(h, h[q != j]))
                if len(free):
                    p = int(rng.choice(free)); t[(r + 1) % N, g, :15, int(h[p])] = v[r, g, :15, p]
    return pack(v, t, w, k)
def setup_inputs_small(rng):
    v, t, w, k = parts(rng)
    return pack(v & 1, t & 1, w, k)
def setup_inputs_spread(rng):
    v, t, w, k = parts(rng); both = []
    for a in (v, t):
        n = a.shape[-1]; b = np.minimum((np.exp2(8 * rng.random((N, 8, 1, n))) * rng.random(a.shape)).astype(np.int64), 127)
        z = rng.integers(0, 32, (N, 8, 1, n)); b = np.where(z == 0, 0, np.where(z == 1, 127, b)); b[:, :, 15] = a[:, :, 15]; both.append(b)
    w = np.minimum(np.exp2(8.1 * rng.random((N, 8, 16))).astype(np.int64), 255); w[:, :, 3] = 0; w[:, :, 4] = 255
    w[:, 5] = rng.integers(200, 256, (N, 16)); w[:, 6] = 255
    both[0][:, 5, :15] = rng.integers(100, 128, (N, 15, P)); both[0][:, 6, :15] = rng.integers(64, 128, (N, 15, P))
    both[0][:, 6, :15, P - 1] = 127; both[0][:, 6, 15, P - 1] = 1
    k = np.minimum(np.exp2(11.1 * rng.random((N, 8, RO, M))).astype(np.int64) - 1, 2047); k[:, 1, 0, 0] = 0; k[:, 2, 0, 1] = 2047
    return pack(both[0], both[1], w, k)
def check_inputs(d):
    bad = []
    for name in ("x", "tm"):
        a = np.asarray(d[name]).astype(np.float32)
        if not np.all((a >= 0) & (a <= 127) & (np.floor(a) == a)): bad.append("whole numbers of " + name)
        if not np.all(a[:, 15::16] <= 1): bad.append("signs of " + name)
    for name, hi in (("wt", 255), ("km", 2047)):
        if np.min(d[name]) < 0 or np.max(d[name]) > hi: bad.append("range of " + name)
    a = np.asarray(d["km"]); a = a.reshape(a.shape[0], 8, 16, -1)
    if not np.all(a == a[:, :, :1]): bad.append("rows of km alike")
    return bad
def reference(x, tm, wt, km):
    v = x.astype(np.float32).astype(np.int32).reshape(N, 8, 16, P); tp = tm.astype(np.float32).astype(np.int32).reshape(N, 8, 16, TW)
    w = wt.astype(np.int32).reshape(N, 8, 16, 1); k = km.astype(np.int32).reshape(N, 8, 16, RO, M)[:, :, 0]; j = np.arange(P)
    for t in range(RO):
        u = np.add.reduce(w * v, axis=2, dtype=np.int32) & 4095
        bq = bd = None
        for m in range(M):
            q = ((u * u >> 5) + k[:, :, t, m][:, :, None] * u) & (P - 1)
            xq = np.take_along_axis(v, q[:, :, None, :], 3)
            dm = np.where(q == j, 8192, np.add.reduce(np.abs(v - xq)[:, :, :15], axis=2))
            if m == 0: bq, bd = q, dm
            else: bq, bd = np.where(dm < bd, q, bq), np.minimum(bd, dm)
        xq = np.take_along_axis(v, bq[:, :, None, :], 3)
        h = (u * np.take_along_axis(u, bq, 2) >> 4) & (TW - 1)
        got = np.stack([np.take_along_axis(tp[(r + 1 + t % (N - 1)) % N], h[r][:, None, :], 2) for r in range(N)])
        e = bd + np.add.reduce(np.abs(v + xq - 2 * got)[:, :, :15], axis=2)
        alike = v[:, :, 15] == xq[:, :, 15]; lo = np.minimum(j, bq); hi = np.maximum(j, bq)
        nv = np.empty_like(v)
        for r in range(N):
            for g in range(8):
                p = int(np.argmin(e[r, g])); a, b = int(lo[r, g, p]), int(hi[r, g, p])
                z = v[r, g].copy(); z[:15, a] = (v[r, g, :15, a] + v[r, g, :15, b]) >> 1
                tp[r, g, :, int(h[r, g, p])] = z[:, a]
                if not alike[r, g, p]:
                    z[:, a + 1:b + 1] = z[:, a + 1:b + 1][:, ::-1].copy(); z[15, a + 1:b + 1] = 1 - z[15, a + 1:b + 1]
                else:
                    c, d = b, P - 1
                    inside = alike[r, g] & (lo[r, g] > a) & (lo[r, g] < b)
                    if np.any(inside):
                        p2 = int(np.argmin(np.where(inside, e[r, g], 2 ** 20)))
                        if hi[r, g, p2] > b: c, d = int(lo[r, g, p2]), int(hi[r, g, p2])
                    z = z[:, np.concatenate([j[:a + 1], j[b + 1:d + 1], j[c + 1:b + 1], j[a + 1:c + 1], j[d + 1:]])]
                nv[r, g] = z
        v = nv
    return {"y": v.reshape(N, 128, P).astype(np.float32).astype(BF)}

@@ -1,0 +1,451 @@
+from concourse.bass import DstId, RemoteDMATransfer
+from concourse.mybir import AluOpType, AxisListType, ActivationFunctionType
+
+OP, AF = AluOpType, ActivationFunctionType
+P, TW, M, RO, NR = 2048, 2048, 3, 5, 4
+NC = P // 16
+CH = [(0, 32), (32, 32), (64, 32), (96, 32)]
+SELF_D = 1920
+SPX = 2 * P
+BIG = float(2 ** 24)
+UE = 2
+SENDS = {0: (1, 2, 3), 1: (1, 2, 3), 2: (1, 2), 3: (2,)}
+CY, GA, FIX, WAKE = .00083, 1.5, .03, .08
+PE = [.0006]
+
+SCRATCH = {}
+for _d, _l in {
+    "float32": "xf 2048 cf 32 kmf 16 grp 128 m16 16 emn 128 nt 128 nt8 128 ntm 128 pt 128 v3 384 vmn 128 b4 128 bq 128 lo 128 key 128 "
+               "lod 128 prd 128 prh 128 prk 128 k2a 128 k2 128 rn 128 md1 128 bs 128 y1 128 g2 128 sf 128 nb2 128 dg 16 dg2 16 c 64 nc 16 "
+               "upd 64 land 192",
+    "bfloat16": "xa 4112 xb 4112 tmo 2048 tb1 2064 tb2 2064 tb3 2064 xq 2048 ag 2048 az 2048 yb 2048 bm 2048 wb 2048 mf 2048 mz 2048 "
+                "idn 128 idf 128 idj 128 idk 128 ids 128 idc 128 id1 128 id2 128 em 128 one 64 eqb 384 sg 128 nd 16",
+    "float16": "mn 6144 md 2048",
+    "int32": "io2 2048 ic 128 ipart 4 ci 16 wti 4 kmi 16 tmpi 128 tmpj 128 ui 128 u 128 sq 128 s5 128 t3 384 q3 384 vm 128 qs 128 b1 128 "
+             "ri 128 uq 128 hp 128 hs 128 ki 128 kv 128 cii 16",
+    "uint16": "l3 384 lq 128 lh 128 ls 128 l1 16"}.items():
+    _w = _l.split()
+    for _i in range(0, len(_w), 2):
+        SCRATCH[_w[_i]] = ("sbuf", [128, int(_w[_i + 1])], _d)
+PSUMS = ["ps0", "ps1", "ps2", "ps3", "ps5", "z0", "z1", "z2"]
+for _n in PSUMS:
+    SCRATCH[_n] = ("psum", [128, 512], "float32")
+SEMAPHORES = ["qv", "qs", "qp", "qg", "dx0", "dx1", "dw", "dk", "dt", "dy0", "dy1", "ls", "tma1", "tma2", "tma3"] + \
+             ["ua%d_%d" % (t, o) for t in SENDS for o in SENDS[t]]
+
+
+def rank_program(g, core, T, topo):
+    rank = T.rank_of(core)
+    if rank is None:
+        return
+    cores = T.cores
+    Q = {"v": g.vector, "s": g.scalar, "p": g.tensor, "g": g, "y": g.sync}
+    QS = {"v": "qv", "s": "qs", "p": "qp", "g": "qg"}
+    ops, wr, rd = [], {}, {}
+
+    def A(n, a=0, b=None, st=1):
+        b = T[n].shape[-1] if b is None else b
+        return (T[n][:, a:b] if st == 1 else T[n][:, a:b:st], [(n, a, b)], (b - a + st - 1) // st)
+
+    def IND(w, o):
+        return (w[0].indirect(o[0]), w[1] + o[1], -16 * o[2])
+
+    def note(q, fn, outs, ins, cost, sem="", inc=1, lat=0.0, ev=None, after=()):
+        me, pre = len(ops), set(after)
+        R = [(r, 0) for o in ins for r in o[1]] + [(r, 1) for o in outs for r in o[1]]
+        for (n, a, b), k in R:
+            for d, w2 in ((wr, 1), (rd, 0)):
+                for a2, b2, q2, i2 in d.setdefault(n, []):
+                    if (n in PSUMS and q2 != q) or (a < b2 and a2 < b and (k or w2)):
+                        pre.add(i2)
+        for (n, a, b), k in R:
+            if k and n not in PSUMS:
+                for d in (wr, rd):
+                    d[n] = [x for x in d[n] if not (a <= x[0] and x[1] <= b)]
+            (wr if k else rd)[n].append((a, b, q, me))
+        pre.discard(me)
+        ops.append(dict(q=q, fn=fn, pre=sorted(pre), cost=cost, sem=sem, inc=inc, lat=lat, ev=ev))
+        return me
+
+    def vcost(o, ins, two=False, half=False):
+        n = max([x[2] for x in ins] + [o[2]])
+        for x in ins + [o]:
+            if x[2] < 0: return -x[2] * CY * (GA if x is not o else 3) + FIX + .05
+        ps = any(x[1][0][0] in PSUMS for x in ins)
+        if two and not ps: n *= 2
+        if half and not ps and all(SCRATCH.get(x[1][0][0], ("", "", ""))[2] in ("bfloat16", "float16", "uint16") for x in ins + [o]): n //= 2
+        return max(64, n) * CY + FIX
+
+    def TT(o, x, y, op):
+        note("v", lambda: g.vector.tensor_tensor(o[0], x[0], y[0], op), [o], [x, y], vcost(o, [x, y], two=True))
+
+    def TS(o, x, s1, op0, s2=None, op1=None):
+        ins = [x] + [s for s in (s1, s2) if isinstance(s, tuple)]
+        v1 = s1[0] if isinstance(s1, tuple) else s1
+        v2 = s2[0] if isinstance(s2, tuple) else s2
+        if op1 is None:
+            note("v", lambda: g.vector.tensor_scalar(o[0], x[0], v1, None, op0), [o], ins, vcost(o, [x], half=True))
+        else:
+            note("v", lambda: g.vector.tensor_scalar(o[0], x[0], v1, v2, op0, op1), [o], ins, vcost(o, [x], half=True))
+
+    def CP(o, x):
+        note("v", lambda: g.vector.tensor_copy(o[0], x[0]), [o], [x], vcost(o, [x], half=True))
+
+    def RED(o, x, op):
+        note("v", lambda: g.vector.tensor_reduce(o[0], x[0], AxisListType.X, op), [o], [x], vcost(o, [x]))
+
+    def FILL(o, v):
+        note("v", lambda: g.vector.memset(o[0], v), [o], [], vcost(o, []))
+
+    def ACT(o, x, func=AF.Copy, bias=None, scale=None):
+        kw = {}
+        if bias is not None: kw["bias"] = bias[0]
+        if scale is not None: kw["scale"] = scale[0] if isinstance(scale, tuple) else scale
+        note("s", lambda: g.scalar.activation(o[0], x[0], func, **kw), [o],
+             [x] + [s for s in (bias, scale) if isinstance(s, tuple)], vcost(o, [x]) + .015)
+
+    def MM(o, pairs, start=True, stop=True):
+        def go():
+            for i, z in enumerate(pairs):
+                k = g.tensor.matmul((z[2] if len(z) > 2 else o)[0], z[0][0], z[1][0], start and i == 0, stop and i == len(pairs) - 1)
+            return k
+        f = [max(64, z[1][2]) * PE[0] * (4 if SCRATCH[z[0][1][0][0]][2] == "float32" else 1) for z in pairs]
+        note("p", go, [o], [y for z in pairs for y in z[:2]], sum(f), lat=.06)
+
+    def DMA(q, o, x, sem):
+        note(q, lambda: Q[q].dma_start(o[0], x[0]), [o], [x], .1, sem, 16, 4.0)
+
+    def SUMS(mat, buf, base, n):
+        return [(A(mat, jj * 128, jj * 128 + 128), A(buf, base + jj, base + 16 * n, 16)) for jj in range(16)]
+
+    def IOTA(pattern, b, cm):
+        note("g", lambda: g.iota(b[0], pattern, 0, cm), [b], [], .13 + 2 * b[2] * CY)
+
+    def H(ap):
+        return (ap, [], 0)
+
+    DMA("y", A("wti", 0, 1), H(T.wt[:]), "dw")
+    DMA("y", A("xa", 0, P // 2), H(T.x[:, 0:P // 2]), "dx0")
+    DMA("s", A("tmo"), H(T.tm[:]), "dt")
+    DMA("y", A("xa", P // 2, P), H(T.x[:, P // 2:P]), "dx1")
+    DMA("y", A("kmi", 0, 15), H(T.km[:]), "dk")
+
+    IOTA([[0, 1]], A("ipart", 0, 1), 1)
+    IOTA([[1, 128]], A("ic"), 0)
+    IOTA([[-1000, 16], [1, 8], [1000, 16]], A("io2"), 0)
+    C = lambda i: A("cf", i, i + 1)
+    JJ, GK, IPF, F15, R15N, FIRST, NF, ODD, MH, SX, ST, CW, CMD, CMF, CMZ, CJ, CK, CB, CTH, CC2, C2047 = [C(i) for i in range(21)]
+    TS(A("ci", 0, 1), A("ipart", 0, 1), 15, OP.bitwise_and)
+    TS(A("ci", 1, 2), A("ipart", 0, 1), 4, OP.arith_shift_right)
+    TS(A("ci", 2, 3), A("ipart", 0, 1), 1, OP.bitwise_and)
+    CP(JJ, A("ci", 0, 1)); CP(GK, A("ci", 1, 2)); CP(ODD, A("ci", 2, 3)); CP(IPF, A("ipart", 0, 1))
+    TS(F15, JJ, 15.0, OP.is_lt)
+    TS(FIRST, JJ, 0.0, OP.is_equal)
+    TS(NF, JJ, 0.0, OP.is_gt)
+    CP(CW, A("wti", 0, 1))
+    TS(CMD, F15, -8192.0, OP.mult, -8192.0, OP.add)
+    TS(CMF, F15, 8192.0, OP.mult)
+    TS(CMZ, F15, 2047.0, OP.mult, 1.0, OP.add)
+    TS(CJ, F15, 2.0, OP.mult, -1.0, OP.add)
+    TS(CK, F15, -2.0, OP.mult)
+    TS(R15N, F15, 1.0, OP.mult, -1.0, OP.add)
+    TS(CB, R15N, -1.0, OP.mult)
+    TS(MH, F15, 0.5, OP.mult)
+    TS(SX, JJ, float(SPX), OP.add, NF, OP.mult)
+    TS(ST, JJ, float(TW), OP.add, NF, OP.mult)
+    FILL(CTH, -8192.0 * (SELF_D - 7)); FILL(CC2, 1024.0 * SELF_D); FILL(C2047, 2047.0)
+    TS(A("idn"), A("ic"), IPF, OP.is_equal)
+    TS(A("tmpi"), A("ic"), 4, OP.arith_shift_right)
+    TS(A("grp"), A("tmpi"), GK, OP.is_equal)
+    TS(A("tmpj"), A("ic"), 15, OP.bitwise_and)
+    TS(A("emn"), A("tmpj"), 15.0, OP.is_equal, F15, OP.mult)
+    TT(A("prd"), A("emn"), A("grp"), OP.mult)
+    TS(A("idf"), A("idn"), F15, OP.mult)
+    TT(A("em"), A("idf"), A("prd"), OP.subtract)
+    TS(A("bm"), A("io2"), GK, OP.is_equal)
+    TS(A("wb"), A("bm"), CW, OP.mult)
+    ACT(A("mf"), A("bm"), AF.Copy, None, CMF)
+    TS(A("md"), A("bm"), CMD, OP.mult)
+    ACT(A("mz"), A("bm"), AF.Copy, None, CMZ)
+    CP(A("kmf", 0, 15), A("kmi", 0, 15))
+    TS(A("nt"), A("ic"), 16.0, OP.mult, JJ, OP.add)
+    TS(A("nt8"), A("nt"), 8.0, OP.mult, -8192.0, OP.add)
+    TS(A("ntm"), A("nt"), -2047.0, OP.add)
+    PL = A("ps0", 0, 128)
+    CP(PL, A("nt"))
+    TS(A("idj"), A("idn"), CJ, OP.mult)
+    TS(A("idk"), A("idn"), CK, OP.mult)
+    TS(A("ids"), A("idn"), float(SELF_D * 8192), OP.mult)
+    TS(A("idc"), A("idn"), float(SELF_D * 1024), OP.mult)
+    TS(A("id1"), A("idn"), 2048.0, OP.mult)
+    TS(A("id2"), A("idn"), 4096.0, OP.mult)
+    TS(A("m16"), A("ic", 0, 16), JJ, OP.is_equal)
+    FILL(A("one"), 1.0); FILL(A("nd"), 0.0); FILL(A("upd"), 0.0)
+    sent, arrived = [0], {}
+
+    def send_table(o):
+        d = cores[(rank - o) % NR]
+        rid, pid = topo.addr(d, core)
+        sent[0] += len(topo.engines(core, d))
+        arrived["tma%d" % o] = len(topo.engines(cores[(rank + o) % NR], core))
+        k = note("g", lambda: g.remote_dma(T["tb%d" % o][:, 0:TW], T.tmo[:], T.sem["tma%d" % o], T.sem.ls, pid, rid, topo.mask(core, d)),
+                 [], [A("tmo")], .5, None)
+        note("x", None, [A("tb%d" % o, 0, TW)], [], 0, None, 1, 4.0 + 6 * o, ("tma%d" % o, arrived["tma%d" % o]), (k,))
+    for o in (1, 2, 3): send_table(o)
+
+    cc = lambda i: A("c", i, i + 1)
+    ii = lambda i: A("cii", i, i + 1)
+    seen, landed = set(), {}
+
+    def updates(t):
+        o = 1 + t % 3
+        for t0 in range(t):
+            if (t0, o) in landed and (t0, o) not in seen:
+                seen.add((t0, o))
+                k = landed[(t0, o)]
+                L = A("l1", 4 + 2 * (len(seen) % 2), 5 + 2 * (len(seen) % 2))
+                TS(L, A("land", 16 * k + 1, 16 * k + 2), FIRST, OP.mult, ST, OP.add)
+                CP(IND(A("tb%d" % o), L), A("land", 16 * k, 16 * k + 16))
+
+    def send_new(t):
+        dsts = [cores[(rank - o) % NR] for o in SENDS[t]]
+        en = [e for e in topo.engines(core, dsts[0]) if all(e in topo.engines(core, d) for d in dsts)]
+        xs = []
+        for i, o in enumerate(SENDS[t]):
+            rid, pid = topo.addr(dsts[i], core)
+            k = len(landed)
+            landed[(t, o)] = k
+            xs.append(RemoteDMATransfer(dst_ids=[DstId(rid=rid, pnc=pid)], dma_engine_mask=sum(1 << e for e in en[UE * i:UE * i + UE]),
+                                        remote_sem=T.sem["ua%d_%d" % (t, o)], src=T.upd[:, 16 * t:16 * t + 16],
+                                        dst=T.land[:, 16 * k:16 * k + 16]))
+            sent[0] += UE
+            arrived["ua%d_%d" % (t, o)] = UE
+        me = note("g", lambda: g.remote_dma_fused(xs, local_sem=T.sem.ls), [], [A("upd", 16 * t, 16 * t + 16)], .5, None)
+        for o in SENDS[t]:
+            k = landed[(t, o)]
+            note("x", None, [A("land", 16 * k, 16 * k + 16)], [], 0, None, 1, 6.0, ("ua%d_%d" % (t, o), UE), (me,))
+
+    def one_round(t):
+        X, XN = ("xa", "xb") if t % 2 == 0 else ("xb", "xa")
+        TB = "tb%d" % (1 + t % 3)
+        MM(A("ps1", 0, 128), SUMS("wb", X, 0, NC))
+        for k in range(4):
+            b = A(["z2", "z0", "z1", "ps2"][k])
+            MM(b, [(A("em"), A(X, 512 * k, 512 * k + 512))])
+            ACT(A("xf", 512 * k, 512 * k + 512), b, AF.Identity, R15N)
+        for k in range(4):
+            ACT(A(X, P + 512 * k, P + 512 * k + 512), A(X, 512 * k, 512 * k + 512), AF.Identity, CB, CJ)
+        MM(A("ps5", 0, 128), SUMS("mf", X, 0, NC))
+        CP(A("ui"), A("ps1", 0, 128))
+        TS(A("u"), A("ui"), 4095, OP.bitwise_and)
+        TT(A("sq"), A("u"), A("u"), OP.mult)
+        TS(A("s5"), A("sq"), 5, OP.arith_shift_right)
+        for m in range(M):
+            a, b = 128 * m, 128 * m + 128
+            TS(A("ps0", a + 128, b + 128), A("u"), A("kmf", 3 * t + m, 3 * t + m + 1), OP.mult)
+            TT(A("t3", a, b), A("s5"), A("ps0", a + 128, b + 128), OP.add)
+            TS(A("q3", a, b), A("t3", a, b), P - 1, OP.bitwise_and)
+            CP(A("l3", a, b), A("q3", a, b))
+            TT(A("eqb", a, b), A("q3", a, b), PL, OP.is_equal)
+        TT(A("pt"), A("nt8"), A("ps5", 0, 128), OP.add)
+
+        def V(m, c):
+            return A("v3", 128 * m + c[0], 128 * m + c[0] + c[1])
+
+        def near(c):
+            c0, n = c
+            a = 16 * c0
+            o0, o1 = A("ps2", 0, n), A("ps2", n, 2 * n)
+            for m in range(M):
+                TT(A("mn", 3 * a + 16 * n * m, 3 * a + 16 * n * (m + 1)), IND(A("xf"), A("l3", 128 * m + c0, 128 * m + c0 + n)),
+                   A(X, a, a + 16 * n), OP.min)
+            MM(A("ps2", 0, 2 * n), SUMS("md", "mn", 48 * c0, 2 * n) +
+               [(A("ids"), A("eqb", c0, c0 + n), o0), (A("ids"), A("eqb", 128 + c0, 128 + c0 + n), o1), (A("id1"), A("one", 0, n), o1)])
+            MM(A("ps3", 0, n), SUMS("md", "mn", 48 * c0 + 32 * n, n) +
+               [(A("ids"), A("eqb", 256 + c0, 256 + c0 + n)), (A("id2"), A("one", 0, n))])
+            for m in (0, 1):
+                TT(V(m, c), A("q3", 128 * m + c0, 128 * m + c0 + n), A("ps2", m * n, m * n + n), OP.add)
+            TT(A("vmn", c0, c0 + n), V(0, c), V(1, c), OP.min)
+            TT(V(2, c), A("q3", 256 + c0, 256 + c0 + n), A("ps3", 0, n), OP.add)
+
+        def choose(c):
+            a, b, n = c[0], c[0] + c[1], c[1]
+            TT(A("vm", a, b), A("vmn", a, b), V(2, c), OP.min)
+            TS(A("qs", a, b), A("vm", a, b), P - 1, OP.bitwise_and)
+            CP(A("lq", a, b), A("qs", a, b))
+            ACT(A("xq", 16 * a, 16 * b), IND(A(X, 0, P), A("lq", a, b)), AF.Copy)
+            MM(A("ps5", 128, 128 + n), SUMS("wb", "xq", 16 * a, n))
+            TS(A("b1", a, b), A("vm", a, b), -8192, OP.bitwise_and)
+            TT(A("b4", a, b), A("b1", a, b), A("pt", a, b), OP.add)
+            ACT(A("sg", a, b), A("b4", a, b), AF.Sign, CTH)
+            ACT(A("bq", a, b), A("b4", a, b), AF.Identity, CC2, 0.25)
+
+        def asked(c, i):
+            a, b, n = c[0], c[0] + c[1], c[1]
+            CP(A("ri", a, b), A("ps5", 128, 128 + n))
+            TS(A("uq", a, b), A("ri", a, b), 4095, OP.bitwise_and)
+            TT(A("hp", a, b), A("uq", a, b), A("u", a, b), OP.mult)
+            TS(A("hs", a, b), A("hp", a, b), 4, OP.arith_shift_right, TW - 1, OP.bitwise_and)
+            CP(A("lh", a, b), A("hs", a, b))
+            z = A("z%d" % (i % 3), 0, 16 * n)
+            MM(z, [(A("idj"), A(X, 16 * a, 16 * b)), (A("idn"), A("xq", 16 * a, 16 * b))], True, False)
+            ACT(A("ag", 16 * a, 16 * b), IND(A(TB, 0, TW), A("lh", a, b)), AF.Copy)
+            MM(z, [(A("idk"), A("ag", 16 * a, 16 * b))], False, True)
+            ACT(A("az", 16 * a, 16 * b), z, AF.Abs)
+
+        def keyed(c):
+            a, b = c[0], c[0] + c[1]
+            MM(A("ps1", a, b), SUMS("mz", "az", 16 * a, c[1]) + [(A("idc"), A("sg", a, b))])
+            TT(A("key", a, b), A("bq", a, b), A("ps1", a, b), OP.add)
+
+        updates(t)
+        for i, c in enumerate(CH):
+            near(c)
+            choose(c)
+            asked(c, i)
+        for c in CH: keyed(c)
+        TT(A("lo"), A("qs"), PL, OP.min)
+
+        def lowest(src, out, dg):
+            RED(out, src, OP.min)
+            TS(A(dg), A("m16"), out, OP.mult)
+            MM(A("ps1", 0, 16), [(A("grp"), A(dg))])
+
+        AC, BC, INV, NIN, BA, B1, B1I, RD, SL, BS, AB, RI = [cc(i) for i in range(10, 22)]
+        E0, E1, E2 = [A("ps0", 128 * m + 128, 128 * m + 256) for m in range(3)]
+        lowest(A("key"), cc(0), "dg")
+        CP(A("ki"), A("key"))
+        TS(A("kv"), A("ki"), 1, OP.bitwise_and)
+        TS(E0, A("kv"), -4096.0, OP.mult)
+        TT(A("lod"), A("lo"), E0, OP.add)
+        RED(cc(1), A("ps1", 0, 16), OP.min)
+        TS(E1, A("key"), cc(1), OP.is_equal)
+        TT(A("prd"), A("qs"), E1, OP.mult)
+        RED(cc(2), A("prd"), OP.add)
+        MM(A("ps1", 0, 1), [(A("grp"), cc(2))])
+        CP(ii(0), cc(1))
+        TS(ii(1), ii(0), 1, OP.arith_shift_right, P - 1, OP.bitwise_and)
+        TS(ii(2), ii(0), 1, OP.bitwise_and)
+        CP(INV, ii(2))
+        TS(NIN, INV, -1.0, OP.mult, 1.0, OP.add)
+        TT(AC, ii(1), A("ps1", 0, 1), OP.min)
+        TT(BC, ii(1), A("ps1", 0, 1), OP.max)
+        TS(E0, A("lod"), AC, OP.is_le, BIG, OP.mult)
+        TT(A("k2a"), A("key"), E0, OP.max)
+        TS(E2, A("lod"), BC, OP.is_ge, BIG, OP.mult)
+        TT(A("k2"), A("k2a"), E2, OP.max)
+        lowest(A("k2"), cc(3), "dg2")
+        RED(cc(4), A("ps1", 0, 16), OP.min)
+        TS(E0, A("k2"), cc(4), OP.is_equal)
+        TT(A("prk"), A("qs"), E0, OP.mult)
+        RED(cc(5), A("prk"), OP.add)
+        MM(A("ps1", 0, 1), [(A("grp"), cc(5))])
+        CP(ii(4), cc(4))
+        TS(ii(5), ii(4), 1, OP.arith_shift_right, P - 1, OP.bitwise_and)
+        TS(cc(6), cc(4), BIG, OP.is_lt, NIN, OP.mult)
+        ACT(BA, AC, AF.Identity, BC, -1.0)
+        ACT(RD, BA, AF.Copy, None, NIN)
+        ACT(RI, INV, AF.Identity, RD, float(P + 1))
+        ACT(AB, AC, AF.Identity, BC)
+        ACT(BS, AB, AF.Identity, RI, INV)
+        ACT(SL, INV, AF.Copy, None, -2.0)
+        ACT(A("rn"), A("nt"), AF.Identity, BS, SL)
+        ACT(A("nb2"), A("ntm"), AF.Identity, BA)
+        ACT(B1, BC, AF.Identity, C2047, -1.0)
+        ACT(B1I, B1, AF.Copy, None, NIN)
+        TS(A("l1", 0, 1), ODD, BA, OP.mult, AC, OP.add)
+        ACT(A("nc"), IND(A(X, 0, P), A("l1", 0, 1)), AF.Copy)
+        TS(A("l1", 2, 3), FIRST, AC, OP.mult, SX, OP.add)
+        TS(cc(22), A("nc", 1, 2), A("nc", 0, 1), OP.subtract, MH, OP.mult)
+        TS(ii(6), cc(22), A("nc", 0, 1), OP.add, -0.25, OP.add)
+        CP(A("nd", 0, 1), ii(6))
+        CP(IND(A(X), A("l1", 2, 3)), A("nd"))
+        TS(A("md1"), A("nt"), AC, OP.is_gt)
+        TS(E2, A("nt"), BC, OP.is_gt, INV, OP.mult)
+        TT(E2, A("md1"), E2, OP.subtract)
+        TT(E2, A("rn"), E2, OP.mult)
+        TT(A("bs"), A("nt"), E2, OP.add)
+        TT(cc(8), ii(5), A("ps1", 0, 1), OP.max)
+        TT(cc(7), ii(5), A("ps1", 0, 1), OP.min)
+        TS(cc(9), cc(8), BC, OP.is_gt, cc(6), OP.mult)
+        TS(cc(24), cc(8), 2047.0, OP.subtract, cc(9), OP.mult)
+        TS(cc(23), cc(7), BC, OP.subtract, cc(9), OP.mult)
+        TT(cc(25), cc(24), cc(23), OP.subtract)
+        TT(cc(26), cc(25), B1I, OP.add)
+        TS(E0, A("nb2"), cc(25), OP.is_gt, RD, OP.mult)
+        TS(E2, A("ntm"), cc(24), OP.is_gt, cc(26), OP.mult)
+        TS(A("g2"), A("nb2"), cc(24), OP.is_gt, cc(26), OP.mult)
+        TT(A("y1"), A("bs"), E0, OP.subtract)
+        TT(E2, A("g2"), E2, OP.subtract)
+        TT(A("sf"), A("y1"), E2, OP.subtract)
+        CP(A("ls"), A("sf"))
+        Y = "yb" if t == RO - 1 else XN
+        for k in (0, 1):
+            CP(A(Y, 512 * k, 512 * k + 512), IND(A(X, 0, 2 * P), A("ls", 32 * k, 32 * k + 32)))
+            ACT(A(Y, 1024 + 512 * k, 1536 + 512 * k), IND(A(X, 0, 2 * P), A("ls", 64 + 32 * k, 96 + 32 * k)), AF.Copy)
+        if t == RO - 1:
+            DMA("y", H(T.y[:, 0:P // 2]), A("yb", 0, P // 2), "dy0")
+            DMA("s", H(T.y[:, P // 2:P]), A("yb", P // 2, P), "dy1")
+            return
+        TT(A("prh"), A("hs"), E1, OP.mult)
+        RED(cc(27), A("prh"), OP.add)
+        MM(A("ps3", 64, 65), [(A("grp"), cc(27))])
+        CP(A("upd", 16 * t, 16 * t + 1), ii(6))
+        CP(A("upd", 16 * t + 1, 16 * t + 2), A("ps3", 64, 65))
+        send_new(t)
+
+    for t in range(RO):
+        one_round(t)
+
+    n = len(ops)
+    post, left, tail = [[] for _ in ops], [len(o["pre"]) for o in ops], [0.0] * n
+    for i in range(n - 1, -1, -1):
+        o = ops[i]
+        for j in o["pre"]: post[j].append(i)
+        tail[i] = o["cost"] + o["lat"] + WAKE + max([tail[j] for j in post[i]] + [0.0])
+    ready, free, at, order = {}, {}, [0.0] * n, []
+    for i in range(n):
+        if not left[i]: ready.setdefault(ops[i]["q"], []).append(i)
+    while len(order) < n:
+        best = None
+        for q in sorted(ready):
+            if ready[q]:
+                st = lambda i: at[i] if q == "x" else max(at[i], free.get(q, 0.0))
+                s0 = min(st(i) for i in ready[q])
+                i = max([i for i in ready[q] if st(i) <= s0 + .05], key=lambda i: (tail[i], -i))
+                if best is None or st(i) < best[0]: best = (st(i), q, i)
+        s0, q, i = best
+        ready[q].remove(i)
+        order.append(i)
+        free[q] = s0 + ops[i]["cost"]
+        for j in post[i]:
+            at[j] = max(at[j], free[q] + ops[i]["lat"] + WAKE)
+            left[j] -= 1
+            if not left[j]: ready.setdefault(ops[j]["q"], []).append(j)
+
+    clk, total, evs = {q: {} for q in list(Q) + ["x"]}, dict(arrived), {}
+    for i in order:
+        o, q, need = ops[i], ops[i]["q"], {}
+        if q == "x":
+            evs[i] = (o["ev"], {})
+            continue
+        for j in o["pre"]:
+            if evs[j] is not None:
+                (s, v), snap = evs[j]
+                if clk[q].get(s, 0) < v and need.get(s, (0,))[0] < v: need[s] = (v, snap)
+        items = sorted(need.items())
+        for s, (v, snap) in items:
+            if not any(s2 != s and sn2.get(s, 0) >= v for s2, (v2, sn2) in items): Q[q].wait_ge(T.sem[s], v)
+        for s, (v, snap) in items:
+            for s2, v2 in list(snap.items()) + [(s, v)]: clk[q][s2] = max(clk[q].get(s2, 0), v2)
+        call = o["fn"]()
+        if o["sem"] is None:
+            evs[i] = None
+            continue
+        s = o["sem"] or QS[q]
+        call.then_inc(T.sem[s], o["inc"])
+        total[s] = total.get(s, 0) + o["inc"]
+        evs[i] = ((s, total[s]), dict(clk[q]))
+    total["ls"] = sent[0]
+    for s in sorted(total):
+        g.wait_ge(T.sem[s], total[s])

@@ -4,23 +4,25 @@ from concourse.mybir import AluOpType, AxisListType, ActivationFunctionType
 OP, AF = AluOpType, ActivationFunctionType
 P, TW, M, RO, NR = 2048, 2048, 3, 5, 4
 NC = P // 16
-CH = [(0, 32), (32, 32), (64, 32), (96, 32)]
+CH = [(0, 64), (64, 64)]
+SM = [0]
+SPL = [0, 1]
 SELF_D = 1920
 SPX = 2 * P
 BIG = float(2 ** 24)
-UE = 2
 SENDS = {0: (1, 2, 3), 1: (1, 2, 3), 2: (1, 2), 3: (2,)}
 CY, GA, FIX, WAKE = .00083, 1.5, .03, .08
-PE = [.0006]
+PE, BON, LATE = [.0006], 1.0, 7.0
 
 SCRATCH = {}
 for _d, _l in {
-    "float32": "xf 2048 cf 32 kmf 16 grp 128 m16 16 emn 128 nt 128 nt8 128 ntm 128 pt 128 v3 384 vmn 128 b4 128 bq 128 lo 128 key 128 "
-               "lod 128 prd 128 prh 128 prk 128 k2a 128 k2 128 rn 128 md1 128 bs 128 y1 128 g2 128 sf 128 nb2 128 dg 16 dg2 16 c 64 nc 16 "
-               "upd 64 land 192",
+    "float32": "idnf 128 nf 128 xf 2048 cf 32 kmf 16 grp 128 m16 16 emn 128 nt 128 nt8 128 ntm 128 pt 128 v3 128 vmn 128 b4 128 bq 128 "
+               "lo 128 key 128 lod 128 prd 128 prh 128 prk 128 k2a 128 k2 128 rn 128 bs 128 y1 128 g2 128 sf 128 nb2 128 dg 16 dg2 16 "
+               "c 64 nc 16 upd 64 land 192",
     "bfloat16": "xa 4112 xb 4112 tmo 2048 tb1 2064 tb2 2064 tb3 2064 xq 2048 ag 2048 az 2048 yb 2048 bm 2048 wb 2048 mf 2048 mz 2048 "
-                "idn 128 idf 128 idj 128 idk 128 ids 128 idc 128 id1 128 id2 128 em 128 one 64 eqb 384 sg 128 nd 16",
-    "float16": "mn 6144 md 2048",
+                "xs 2048 as 2048 idm 128 ma 128 mb 128 idn 128 idf 128 idj 128 idk 128 ids 128 idc 128 id1 128 id2 128 em 128 one 64 "
+                "eqb 384 sg 128 nd 16",
+    "float16": "mn 6144 md 2048 q16 384 id16 128",
     "int32": "io2 2048 ic 128 ipart 4 ci 16 wti 4 kmi 16 tmpi 128 tmpj 128 ui 128 u 128 sq 128 s5 128 t3 384 q3 384 vm 128 qs 128 b1 128 "
              "ri 128 uq 128 hp 128 hs 128 ki 128 kv 128 cii 16",
     "uint16": "l3 384 lq 128 lh 128 ls 128 l1 16"}.items():
@@ -30,18 +32,17 @@ for _d, _l in {
 PSUMS = ["ps0", "ps1", "ps2", "ps3", "ps5", "z0", "z1", "z2"]
 for _n in PSUMS:
     SCRATCH[_n] = ("psum", [128, 512], "float32")
-SEMAPHORES = ["qv", "qs", "qp", "qg", "dx0", "dx1", "dw", "dk", "dt", "dy0", "dy1", "ls", "tma1", "tma2", "tma3"] + \
+SEMAPHORES = ["qv", "qs", "qp", "qg", "dx0", "dx1", "dw", "dk", "dt", "dy0", "dy1", "dy2", "dy3", "ls", "tma1", "tma2", "tma3"] + \
              ["ua%d_%d" % (t, o) for t in SENDS for o in SENDS[t]]
 
 
 def rank_program(g, core, T, topo):
-    rank = T.rank_of(core)
+    rank, cores = T.rank_of(core), T.cores
     if rank is None:
         return
-    cores = T.cores
     Q = {"v": g.vector, "s": g.scalar, "p": g.tensor, "g": g, "y": g.sync}
     QS = {"v": "qv", "s": "qs", "p": "qp", "g": "qg"}
-    ops, wr, rd = [], {}, {}
+    ops, wr, rd, bon = [], {}, {}, [0.0]
 
     def A(n, a=0, b=None, st=1):
         b = T[n].shape[-1] if b is None else b
@@ -64,7 +65,7 @@ def rank_program(g, core, T, topo):
                     d[n] = [x for x in d[n] if not (a <= x[0] and x[1] <= b)]
             (wr if k else rd)[n].append((a, b, q, me))
         pre.discard(me)
-        ops.append(dict(q=q, fn=fn, pre=sorted(pre), cost=cost, sem=sem, inc=inc, lat=lat, ev=ev))
+        ops.append(dict(q=q, fn=fn, pre=sorted(pre), cost=cost, bon=bon[0], sem=sem, inc=inc, lat=lat, ev=ev))
         return me
 
     def vcost(o, ins, two=False, half=False):
@@ -118,8 +119,8 @@ def rank_program(g, core, T, topo):
     def SUMS(mat, buf, base, n):
         return [(A(mat, jj * 128, jj * 128 + 128), A(buf, base + jj, base + 16 * n, 16)) for jj in range(16)]
 
-    def IOTA(pattern, b, cm):
-        note("g", lambda: g.iota(b[0], pattern, 0, cm), [b], [], .13 + 2 * b[2] * CY)
+    def IOTA(pattern, b, cm, base=0):
+        note("g", lambda: g.iota(b[0], pattern, base, cm), [b], [], .13 + 2 * b[2] * CY)
 
     def H(ap):
         return (ap, [], 0)
@@ -132,9 +133,11 @@ def rank_program(g, core, T, topo):
 
     IOTA([[0, 1]], A("ipart", 0, 1), 1)
     IOTA([[1, 128]], A("ic"), 0)
-    IOTA([[-1000, 16], [1, 8], [1000, 16]], A("io2"), 0)
+    for k in (0, 1):
+        IOTA([[-1000, 8], [1, 8], [1000, 16]], A("io2", 1024 * k, 1024 * k + 1024), 0, -8000 * k)
     C = lambda i: A("cf", i, i + 1)
-    JJ, GK, IPF, F15, R15N, FIRST, NF, ODD, MH, SX, ST, CW, CMD, CMF, CMZ, CJ, CK, CB, CTH, CC2, C2047 = [C(i) for i in range(21)]
+    (JJ, GK, IPF, F15, R15N, FIRST, NF, ODD, MH, SX, ST, CW, CMD, CMF, CMZ, CJ, CK, CB, CTH, CC2, C2047, C8K, CMH2, CQ, CP23, CM23, C1,
+     CM2047) = [C(i) for i in range(28)]
     TS(A("ci", 0, 1), A("ipart", 0, 1), 15, OP.bitwise_and)
     TS(A("ci", 1, 2), A("ipart", 0, 1), 4, OP.arith_shift_right)
     TS(A("ci", 2, 3), A("ipart", 0, 1), 1, OP.bitwise_and)
@@ -151,9 +154,12 @@ def rank_program(g, core, T, topo):
     TS(R15N, F15, 1.0, OP.mult, -1.0, OP.add)
     TS(CB, R15N, -1.0, OP.mult)
     TS(MH, F15, 0.5, OP.mult)
+    TS(CMH2, MH, -1.0, OP.mult, 1.0, OP.add)
     TS(SX, JJ, float(SPX), OP.add, NF, OP.mult)
     TS(ST, JJ, float(TW), OP.add, NF, OP.mult)
-    FILL(CTH, -8192.0 * (SELF_D - 7)); FILL(CC2, 1024.0 * SELF_D); FILL(C2047, 2047.0)
+    for b, v in ((CTH, -8192.0 * (SELF_D - 7)), (CC2, 1024.0 * SELF_D), (C2047, 2047.0), (C8K, 8192.0), (CQ, -0.25),
+                 (CP23, 8388608.0), (CM23, -8388608.0), (C1, 1.0), (CM2047, -2047.0)):
+        FILL(b, v)
     TS(A("idn"), A("ic"), IPF, OP.is_equal)
     TS(A("tmpi"), A("ic"), 4, OP.arith_shift_right)
     TS(A("grp"), A("tmpi"), GK, OP.is_equal)
@@ -162,10 +168,11 @@ def rank_program(g, core, T, topo):
     TT(A("prd"), A("emn"), A("grp"), OP.mult)
     TS(A("idf"), A("idn"), F15, OP.mult)
     TT(A("em"), A("idf"), A("prd"), OP.subtract)
+    for k in (0, 1):
+        TS(A("wb", 1024 * k, 1024 * k + 1024), A("io2", 1024 * k, 1024 * k + 1024), GK, OP.is_equal, CW, OP.mult)
+    TS(A("md"), A("io2"), GK, OP.is_equal, CMD, OP.mult)
     TS(A("bm"), A("io2"), GK, OP.is_equal)
-    TS(A("wb"), A("bm"), CW, OP.mult)
     ACT(A("mf"), A("bm"), AF.Copy, None, CMF)
-    TS(A("md"), A("bm"), CMD, OP.mult)
     ACT(A("mz"), A("bm"), AF.Copy, None, CMZ)
     CP(A("kmf", 0, 15), A("kmi", 0, 15))
     TS(A("nt"), A("ic"), 16.0, OP.mult, JJ, OP.add)
@@ -179,8 +186,12 @@ def rank_program(g, core, T, topo):
     TS(A("idc"), A("idn"), float(SELF_D * 1024), OP.mult)
     TS(A("id1"), A("idn"), 2048.0, OP.mult)
     TS(A("id2"), A("idn"), 4096.0, OP.mult)
+    TS(A("idm"), A("idn"), -1.0, OP.mult)
+    TS(A("id16"), A("ic"), IPF, OP.is_equal)
+    TS(A("idnf"), A("ic"), IPF, OP.is_equal)
     TS(A("m16"), A("ic", 0, 16), JJ, OP.is_equal)
     FILL(A("one"), 1.0); FILL(A("nd"), 0.0); FILL(A("upd"), 0.0)
+
     sent, arrived = [0], {}
 
     def send_table(o):
@@ -207,23 +218,31 @@ def rank_program(g, core, T, topo):
                 TS(L, A("land", 16 * k + 1, 16 * k + 2), FIRST, OP.mult, ST, OP.add)
                 CP(IND(A("tb%d" % o), L), A("land", 16 * k, 16 * k + 16))
 
+    def shares(r, t):
+        src, dst = cores[r], {o: cores[(r - o) % NR] for o in SENDS[t]}
+        away = [o for o in SENDS[t] if dst[o] not in topo.cores_of(src)]
+        off = topo.engines(src, dst[away[0]])
+        w = len(off) // len(away)
+        es = {o: off[i * w:i * w + w] for i, o in enumerate(away)}
+        for o in SENDS[t]:
+            if o not in es: es[o] = [e for e in topo.engines(src, dst[o]) if e not in off]
+        return es
+
     def send_new(t):
-        dsts = [cores[(rank - o) % NR] for o in SENDS[t]]
-        en = [e for e in topo.engines(core, dsts[0]) if all(e in topo.engines(core, d) for d in dsts)]
-        xs = []
-        for i, o in enumerate(SENDS[t]):
-            rid, pid = topo.addr(dsts[i], core)
+        es, xs = shares(rank, t), []
+        for o in SENDS[t]:
+            rid, pid = topo.addr(cores[(rank - o) % NR], core)
             k = len(landed)
             landed[(t, o)] = k
-            xs.append(RemoteDMATransfer(dst_ids=[DstId(rid=rid, pnc=pid)], dma_engine_mask=sum(1 << e for e in en[UE * i:UE * i + UE]),
+            xs.append(RemoteDMATransfer(dst_ids=[DstId(rid=rid, pnc=pid)], dma_engine_mask=sum(1 << e for e in es[o]),
                                         remote_sem=T.sem["ua%d_%d" % (t, o)], src=T.upd[:, 16 * t:16 * t + 16],
                                         dst=T.land[:, 16 * k:16 * k + 16]))
-            sent[0] += UE
-            arrived["ua%d_%d" % (t, o)] = UE
+            sent[0] += len(es[o])
+            arrived["ua%d_%d" % (t, o)] = len(shares((rank + o) % NR, t)[o])
         me = note("g", lambda: g.remote_dma_fused(xs, local_sem=T.sem.ls), [], [A("upd", 16 * t, 16 * t + 16)], .5, None)
         for o in SENDS[t]:
-            k = landed[(t, o)]
-            note("x", None, [A("land", 16 * k, 16 * k + 16)], [], 0, None, 1, 6.0, ("ua%d_%d" % (t, o), UE), (me,))
+            k, s = landed[(t, o)], "ua%d_%d" % (t, o)
+            note("x", None, [A("land", 16 * k, 16 * k + 16)], [], 0, None, 1, LATE, (s, arrived[s]), (me,))
 
     def one_round(t):
         X, XN = ("xa", "xb") if t % 2 == 0 else ("xb", "xa")
@@ -247,38 +266,53 @@ def rank_program(g, core, T, topo):
             TS(A("q3", a, b), A("t3", a, b), P - 1, OP.bitwise_and)
             CP(A("l3", a, b), A("q3", a, b))
             TT(A("eqb", a, b), A("q3", a, b), PL, OP.is_equal)
+            CP(A("q16", a, b), A("q3", a, b))
+        ACT(A("nf"), A("ps5", 0, 128), AF.Identity, C8K, -1.0)
         TT(A("pt"), A("nt8"), A("ps5", 0, 128), OP.add)
 
-        def V(m, c):
-            return A("v3", 128 * m + c[0], 128 * m + c[0] + c[1])
+        def pick(out, tab, lst, a, b, i):
+            for k, h in enumerate(range(a, b, 32)):
+                o, x = A(out, 16 * h, 16 * min(h + 32, b)), IND(A(tab, 0, P), A(lst, h, min(h + 32, b)))
+                if i in SPL and k % 2: CP(o, x)
+                else: ACT(o, x, AF.Copy)
 
-        def near(c):
+        def near(c, i):
             c0, n = c
             a = 16 * c0
+            e = lambda m: A("eqb", 128 * m + c0, 128 * m + c0 + n)
+            k = lambda m: A("q16", 128 * m + c0, 128 * m + c0 + n)
+            l = lambda m: A("l3", 128 * m + c0, 128 * m + c0 + n)
             o0, o1 = A("ps2", 0, n), A("ps2", n, 2 * n)
-            for m in range(M):
-                TT(A("mn", 3 * a + 16 * n * m, 3 * a + 16 * n * (m + 1)), IND(A("xf"), A("l3", 128 * m + c0, 128 * m + c0 + n)),
-                   A(X, a, a + 16 * n), OP.min)
+            for m in range(2 if i in SM else 3):
+                TT(A("mn", 3 * a + 16 * n * m, 3 * a + 16 * n * (m + 1)), IND(A("xf"), l(m)), A(X, a, a + 16 * n), OP.min)
             MM(A("ps2", 0, 2 * n), SUMS("md", "mn", 48 * c0, 2 * n) +
-               [(A("ids"), A("eqb", c0, c0 + n), o0), (A("ids"), A("eqb", 128 + c0, 128 + c0 + n), o1), (A("id1"), A("one", 0, n), o1)])
-            MM(A("ps3", 0, n), SUMS("md", "mn", 48 * c0 + 32 * n, n) +
-               [(A("ids"), A("eqb", 256 + c0, 256 + c0 + n)), (A("id2"), A("one", 0, n))])
-            for m in (0, 1):
-                TT(V(m, c), A("q3", 128 * m + c0, 128 * m + c0 + n), A("ps2", m * n, m * n + n), OP.add)
-            TT(A("vmn", c0, c0 + n), V(0, c), V(1, c), OP.min)
-            TT(V(2, c), A("q3", 256 + c0, 256 + c0 + n), A("ps3", 0, n), OP.add)
+               [(A("ids"), e(0), o0), (A("ids"), e(1), o1), (A("id1"), A("one", 0, n), o1), (A("id16"), k(0), o0), (A("id16"), k(1), o1)])
+            last = [(A("ids"), e(2)), (A("id2"), A("one", 0, n)), (A("id16"), k(2))]
+            if i in SM:
+                for p0 in range(a, a + 16 * n, 512):
+                    p1 = min(p0 + 512, a + 16 * n)
+                    w = A("z2", 0, p1 - p0)
+                    ACT(A("xs", p0, p1), IND(A(X, 0, P), A("l3", 256 + p0 // 16, 256 + p1 // 16)), AF.Copy)
+                    MM(w, [(A("idm"), A(X, p0, p1)), (A("idn"), A("xs", p0, p1))])
+                    ACT(A("as", p0, p1), w, AF.Abs)
+                MM(A("ps3", 0, n), SUMS("mf", "as", a, n) + last + [(A("idnf"), A("nf", c0, c0 + n))])
+            else:
+                MM(A("ps3", 0, n), SUMS("md", "mn", 48 * c0 + 32 * n, n) + last)
+            ACT(A("v3", c0, c0 + n), o0, AF.Copy)
+            TT(A("vmn", c0, c0 + n), A("v3", c0, c0 + n), o1, OP.min)
 
-        def choose(c):
+        def choose(c, i):
             a, b, n = c[0], c[0] + c[1], c[1]
-            TT(A("vm", a, b), A("vmn", a, b), V(2, c), OP.min)
+            TT(A("vm", a, b), A("vmn", a, b), A("ps3", 0, n), OP.min)
             TS(A("qs", a, b), A("vm", a, b), P - 1, OP.bitwise_and)
             CP(A("lq", a, b), A("qs", a, b))
-            ACT(A("xq", 16 * a, 16 * b), IND(A(X, 0, P), A("lq", a, b)), AF.Copy)
+            pick("xq", X, "lq", a, b, i)
             MM(A("ps5", 128, 128 + n), SUMS("wb", "xq", 16 * a, n))
             TS(A("b1", a, b), A("vm", a, b), -8192, OP.bitwise_and)
             TT(A("b4", a, b), A("b1", a, b), A("pt", a, b), OP.add)
             ACT(A("sg", a, b), A("b4", a, b), AF.Sign, CTH)
             ACT(A("bq", a, b), A("b4", a, b), AF.Identity, CC2, 0.25)
+            TT(A("lo", a, b), A("qs", a, b), A("ps0", a, b), OP.min)
 
         def asked(c, i):
             a, b, n = c[0], c[0] + c[1], c[1]
@@ -287,47 +321,59 @@ def rank_program(g, core, T, topo):
             TT(A("hp", a, b), A("uq", a, b), A("u", a, b), OP.mult)
             TS(A("hs", a, b), A("hp", a, b), 4, OP.arith_shift_right, TW - 1, OP.bitwise_and)
             CP(A("lh", a, b), A("hs", a, b))
-            z = A("z%d" % (i % 3), 0, 16 * n)
-            MM(z, [(A("idj"), A(X, 16 * a, 16 * b)), (A("idn"), A("xq", 16 * a, 16 * b))], True, False)
-            ACT(A("ag", 16 * a, 16 * b), IND(A(TB, 0, TW), A("lh", a, b)), AF.Copy)
-            MM(z, [(A("idk"), A("ag", 16 * a, 16 * b))], False, True)
-            ACT(A("az", 16 * a, 16 * b), z, AF.Abs)
+            sg = [(A("z%d" % (k % 2), 0, min(512, 16 * b - p0)), p0, min(p0 + 512, 16 * b)) for k, p0 in enumerate(range(16 * a, 16 * b, 512))]
+            for z, p0, p1 in sg:
+                MM(z, [(A("idj"), A(X, p0, p1)), (A("idn"), A("xq", p0, p1))], True, False)
+            pick("ag", TB, "lh", a, b, i)
+            for z, p0, p1 in sg:
+                MM(z, [(A("idk"), A("ag", p0, p1))], False, True)
+                ACT(A("az", p0, p1), z, AF.Abs)
 
         def keyed(c):
             a, b = c[0], c[0] + c[1]
             MM(A("ps1", a, b), SUMS("mz", "az", 16 * a, c[1]) + [(A("idc"), A("sg", a, b))])
             TT(A("key", a, b), A("bq", a, b), A("ps1", a, b), OP.add)
 
+        AC, BC, INV, NIN, BA, B1, B1I, RD, SL, BS, AB, RI = [cc(i) for i in range(10, 22)]
+        E0, E1, E2 = [A("ps0", 128 * m + 128, 128 * m + 256) for m in range(3)]
         updates(t)
         for i, c in enumerate(CH):
-            near(c)
-            choose(c)
+            bon[0] = BON * (len(CH) - i)
+            near(c, i)
+            choose(c, i)
             asked(c, i)
-        for c in CH: keyed(c)
-        TT(A("lo"), A("qs"), PL, OP.min)
+        for i, c in enumerate(CH):
+            bon[0] = BON * (len(CH) - i)
+            keyed(c)
+            a, b = c[0], c[0] + c[1]
+            e = A("ps0", 128 + a, 128 + b)
+            CP(A("ki", a, b), A("key", a, b))
+            TS(A("kv", a, b), A("ki", a, b), 1, OP.bitwise_and)
+            TS(e, A("kv", a, b), -4096.0, OP.mult)
+            TT(A("lod", a, b), A("lo", a, b), e, OP.add)
+        bon[0] = 0.0
 
         def lowest(src, out, dg):
             RED(out, src, OP.min)
             TS(A(dg), A("m16"), out, OP.mult)
             MM(A("ps1", 0, 16), [(A("grp"), A(dg))])
 
-        AC, BC, INV, NIN, BA, B1, B1I, RD, SL, BS, AB, RI = [cc(i) for i in range(10, 22)]
-        E0, E1, E2 = [A("ps0", 128 * m + 128, 128 * m + 256) for m in range(3)]
         lowest(A("key"), cc(0), "dg")
-        CP(A("ki"), A("key"))
-        TS(A("kv"), A("ki"), 1, OP.bitwise_and)
-        TS(E0, A("kv"), -4096.0, OP.mult)
-        TT(A("lod"), A("lo"), E0, OP.add)
         RED(cc(1), A("ps1", 0, 16), OP.min)
         TS(E1, A("key"), cc(1), OP.is_equal)
         TT(A("prd"), A("qs"), E1, OP.mult)
         RED(cc(2), A("prd"), OP.add)
         MM(A("ps1", 0, 1), [(A("grp"), cc(2))])
+        if t < RO - 1:
+            TT(A("prh"), A("hs"), E1, OP.mult)
+            RED(cc(27), A("prh"), OP.add)
+            MM(A("ps3", 64, 65), [(A("grp"), cc(27))])
+            CP(A("upd", 16 * t + 1, 16 * t + 2), A("ps3", 64, 65))
         CP(ii(0), cc(1))
         TS(ii(1), ii(0), 1, OP.arith_shift_right, P - 1, OP.bitwise_and)
         TS(ii(2), ii(0), 1, OP.bitwise_and)
         CP(INV, ii(2))
-        TS(NIN, INV, -1.0, OP.mult, 1.0, OP.add)
+        ACT(NIN, INV, AF.Identity, C1, -1.0)
         TT(AC, ii(1), A("ps1", 0, 1), OP.min)
         TT(BC, ii(1), A("ps1", 0, 1), OP.max)
         TS(E0, A("lod"), AC, OP.is_le, BIG, OP.mult)
@@ -353,29 +399,38 @@ def rank_program(g, core, T, topo):
         ACT(A("nb2"), A("ntm"), AF.Identity, BA)
         ACT(B1, BC, AF.Identity, C2047, -1.0)
         ACT(B1I, B1, AF.Copy, None, NIN)
+        ACT(cc(32), BC, AF.Identity, CM2047)
         TS(A("l1", 0, 1), ODD, BA, OP.mult, AC, OP.add)
         ACT(A("nc"), IND(A(X, 0, P), A("l1", 0, 1)), AF.Copy)
         TS(A("l1", 2, 3), FIRST, AC, OP.mult, SX, OP.add)
-        TS(cc(22), A("nc", 1, 2), A("nc", 0, 1), OP.subtract, MH, OP.mult)
-        TS(ii(6), cc(22), A("nc", 0, 1), OP.add, -0.25, OP.add)
-        CP(A("nd", 0, 1), ii(6))
+        ACT(cc(22), A("nc", 0, 1), AF.Identity, CQ, CMH2)
+        ACT(cc(28), A("nc", 1, 2), AF.Identity, cc(22), MH)
+        ACT(cc(29), cc(28), AF.Identity, CP23)
+        ACT(A("nd", 0, 1), cc(29), AF.Identity, CM23)
         CP(IND(A(X), A("l1", 2, 3)), A("nd"))
-        TS(A("md1"), A("nt"), AC, OP.is_gt)
-        TS(E2, A("nt"), BC, OP.is_gt, INV, OP.mult)
-        TT(E2, A("md1"), E2, OP.subtract)
-        TT(E2, A("rn"), E2, OP.mult)
+        if t < RO - 1:
+            ACT(A("upd", 16 * t, 16 * t + 1), A("nd", 0, 1), AF.Copy)
+            send_new(t)
+        ACT(cc(30), AC, AF.Copy, None, -1.0)
+        ACT(cc(31), BC, AF.Copy, None, -1.0)
+        ACT(A("ma"), A("nt"), AF.Sign, cc(30))
+        ACT(A("mb"), A("nt"), AF.Sign, cc(31))
+        ACT(A("ma"), A("ma"), AF.Relu)
+        ACT(A("mb"), A("mb"), AF.Relu, None, INV)
+        MM(A("z0", 0, 128), [(A("idn"), A("ma")), (A("idm"), A("mb"))])
+        TT(E2, A("rn"), A("z0", 0, 128), OP.mult)
         TT(A("bs"), A("nt"), E2, OP.add)
         TT(cc(8), ii(5), A("ps1", 0, 1), OP.max)
         TT(cc(7), ii(5), A("ps1", 0, 1), OP.min)
         TS(cc(9), cc(8), BC, OP.is_gt, cc(6), OP.mult)
+        TT(cc(23), cc(8), cc(7), OP.subtract)
+        TS(cc(25), cc(23), cc(32), OP.add, cc(9), OP.mult)
         TS(cc(24), cc(8), 2047.0, OP.subtract, cc(9), OP.mult)
-        TS(cc(23), cc(7), BC, OP.subtract, cc(9), OP.mult)
-        TT(cc(25), cc(24), cc(23), OP.subtract)
         TT(cc(26), cc(25), B1I, OP.add)
         TS(E0, A("nb2"), cc(25), OP.is_gt, RD, OP.mult)
+        TT(A("y1"), A("bs"), E0, OP.subtract)
         TS(E2, A("ntm"), cc(24), OP.is_gt, cc(26), OP.mult)
         TS(A("g2"), A("nb2"), cc(24), OP.is_gt, cc(26), OP.mult)
-        TT(A("y1"), A("bs"), E0, OP.subtract)
         TT(E2, A("g2"), E2, OP.subtract)
         TT(A("sf"), A("y1"), E2, OP.subtract)
         CP(A("ls"), A("sf"))
@@ -384,15 +439,8 @@ def rank_program(g, core, T, topo):
             CP(A(Y, 512 * k, 512 * k + 512), IND(A(X, 0, 2 * P), A("ls", 32 * k, 32 * k + 32)))
             ACT(A(Y, 1024 + 512 * k, 1536 + 512 * k), IND(A(X, 0, 2 * P), A("ls", 64 + 32 * k, 96 + 32 * k)), AF.Copy)
         if t == RO - 1:
-            DMA("y", H(T.y[:, 0:P // 2]), A("yb", 0, P // 2), "dy0")
-            DMA("s", H(T.y[:, P // 2:P]), A("yb", P // 2, P), "dy1")
-            return
-        TT(A("prh"), A("hs"), E1, OP.mult)
-        RED(cc(27), A("prh"), OP.add)
-        MM(A("ps3", 64, 65), [(A("grp"), cc(27))])
-        CP(A("upd", 16 * t, 16 * t + 1), ii(6))
-        CP(A("upd", 16 * t + 1, 16 * t + 2), A("ps3", 64, 65))
-        send_new(t)
+            for k in range(4):
+                DMA("ysys"[k], H(T.y[:, 512 * k:512 * k + 512]), A("yb", 512 * k, 512 * k + 512), "dy%d" % k)
 
     for t in range(RO):
         one_round(t)
@@ -403,6 +451,8 @@ def rank_program(g, core, T, topo):
         o = ops[i]
         for j in o["pre"]: post[j].append(i)
         tail[i] = o["cost"] + o["lat"] + WAKE + max([tail[j] for j in post[i]] + [0.0])
+    pri = list(tail)
+    for i in range(n - 1, -1, -1): pri[i] = max([tail[i] + ops[i]["bon"]] + [pri[j] + ops[i]["cost"] for j in post[i]])
     ready, free, at, order = {}, {}, [0.0] * n, []
     for i in range(n):
         if not left[i]: ready.setdefault(ops[i]["q"], []).append(i)
@@ -412,7 +462,7 @@ def rank_program(g, core, T, topo):
             if ready[q]:
                 st = lambda i: at[i] if q == "x" else max(at[i], free.get(q, 0.0))
                 s0 = min(st(i) for i in ready[q])
-                i = max([i for i in ready[q] if st(i) <= s0 + .05], key=lambda i: (tail[i], -i))
+                i = max([i for i in ready[q] if st(i) <= s0 + .05], key=lambda i: (pri[i], -i))
                 if best is None or st(i) < best[0]: best = (st(i), q, i)
         s0, q, i = best
         ready[q].remove(i)

from concourse.bass import DstId, RemoteDMATransfer
from concourse.mybir import AluOpType, AxisListType, ActivationFunctionType

OP, AF = AluOpType, ActivationFunctionType
P, TW, M, RO, NR = 2048, 2048, 3, 5, 4
NC = P // 16
CH = [(0, 64), (64, 64)]
SM = [0]
SPL = [0, 1]
SELF_D = 1920
SPX = 2 * P
BIG = float(2 ** 24)
SENDS = {0: (1, 2, 3), 1: (1, 2, 3), 2: (1, 2), 3: (2,)}
CY, GA, FIX, WAKE = .00083, 1.5, .03, .08
PE, BON, LATE = [.0006], 1.0, 7.0

SCRATCH = {}
for _d, _l in {
    "float32": "idnf 128 nf 128 xf 2048 cf 32 kmf 16 grp 128 m16 16 emn 128 nt 128 nt8 128 ntm 128 pt 128 v3 128 vmn 128 b4 128 bq 128 "
               "lo 128 key 128 lod 128 prd 128 prh 128 prk 128 k2a 128 k2 128 rn 128 bs 128 y1 128 g2 128 sf 128 nb2 128 dg 16 dg2 16 "
               "c 64 nc 16 upd 64 land 192",
    "bfloat16": "xa 4112 xb 4112 tmo 2048 tb1 2064 tb2 2064 tb3 2064 xq 2048 ag 2048 az 2048 yb 2048 bm 2048 wb 2048 mf 2048 mz 2048 "
                "xs 2048 as 2048 idm 128 ma 128 mb 128 idn 128 idf 128 idj 128 idk 128 ids 128 idc 128 id1 128 id2 128 em 128 one 64 "
                "eqb 384 sg 128 nd 16",
    "float16": "mn 6144 md 2048 q16 384 id16 128",
    "int32": "io2 2048 ic 128 ipart 4 ci 16 wti 4 kmi 16 tmpi 128 tmpj 128 ui 128 u 128 sq 128 s5 128 t3 384 q3 384 vm 128 qs 128 b1 128 "
             "ri 128 uq 128 hp 128 hs 128 ki 128 kv 128 cii 16",
    "uint16": "l3 384 lq 128 lh 128 ls 128 l1 16"}.items():
    _w = _l.split()
    for _i in range(0, len(_w), 2):
        SCRATCH[_w[_i]] = ("sbuf", [128, int(_w[_i + 1])], _d)
PSUMS = ["ps0", "ps1", "ps2", "ps3", "ps5", "z0", "z1", "z2"]
for _n in PSUMS:
    SCRATCH[_n] = ("psum", [128, 512], "float32")
SEMAPHORES = ["qv", "qs", "qp", "qg", "dx0", "dx1", "dw", "dk", "dt", "dy0", "dy1", "dy2", "dy3", "ls", "tma1", "tma2", "tma3"] + \
             ["ua%d_%d" % (t, o) for t in SENDS for o in SENDS[t]]


def rank_program(g, core, T, topo):
    rank, cores = T.rank_of(core), T.cores
    if rank is None:
        return
    Q = {"v": g.vector, "s": g.scalar, "p": g.tensor, "g": g, "y": g.sync}
    QS = {"v": "qv", "s": "qs", "p": "qp", "g": "qg"}
    ops, wr, rd, bon = [], {}, {}, [0.0]

    def A(n, a=0, b=None, st=1):
        b = T[n].shape[-1] if b is None else b
        return (T[n][:, a:b] if st == 1 else T[n][:, a:b:st], [(n, a, b)], (b - a + st - 1) // st)

    def IND(w, o):
        return (w[0].indirect(o[0]), w[1] + o[1], -16 * o[2])

    def note(q, fn, outs, ins, cost, sem="", inc=1, lat=0.0, ev=None, after=()):
        me, pre = len(ops), set(after)
        R = [(r, 0) for o in ins for r in o[1]] + [(r, 1) for o in outs for r in o[1]]
        for (n, a, b), k in R:
            for d, w2 in ((wr, 1), (rd, 0)):
                for a2, b2, q2, i2 in d.setdefault(n, []):
                    if (n in PSUMS and q2 != q) or (a < b2 and a2 < b and (k or w2)):
                        pre.add(i2)
        for (n, a, b), k in R:
            if k and n not in PSUMS:
                for d in (wr, rd):
                    d[n] = [x for x in d[n] if not (a <= x[0] and x[1] <= b)]
            (wr if k else rd)[n].append((a, b, q, me))
        pre.discard(me)
        ops.append(dict(q=q, fn=fn, pre=sorted(pre), cost=cost, bon=bon[0], sem=sem, inc=inc, lat=lat, ev=ev))
        return me

    def vcost(o, ins, two=False, half=False):
        n = max([x[2] for x in ins] + [o[2]])
        for x in ins + [o]:
            if x[2] < 0: return -x[2] * CY * (GA if x is not o else 3) + FIX + .05
        ps = any(x[1][0][0] in PSUMS for x in ins)
        if two and not ps: n *= 2
        if half and not ps and all(SCRATCH.get(x[1][0][0], ("", "", ""))[2] in ("bfloat16", "float16", "uint16") for x in ins + [o]): n //= 2
        return max(64, n) * CY + FIX

    def TT(o, x, y, op):
        note("v", lambda: g.vector.tensor_tensor(o[0], x[0], y[0], op), [o], [x, y], vcost(o, [x, y], two=True))

    def TS(o, x, s1, op0, s2=None, op1=None):
        ins = [x] + [s for s in (s1, s2) if isinstance(s, tuple)]
        v1 = s1[0] if isinstance(s1, tuple) else s1
        v2 = s2[0] if isinstance(s2, tuple) else s2
        if op1 is None:
            note("v", lambda: g.vector.tensor_scalar(o[0], x[0], v1, None, op0), [o], ins, vcost(o, [x], half=True))
        else:
            note("v", lambda: g.vector.tensor_scalar(o[0], x[0], v1, v2, op0, op1), [o], ins, vcost(o, [x], half=True))

    def CP(o, x):
        note("v", lambda: g.vector.tensor_copy(o[0], x[0]), [o], [x], vcost(o, [x], half=True))

    def RED(o, x, op):
        note("v", lambda: g.vector.tensor_reduce(o[0], x[0], AxisListType.X, op), [o], [x], vcost(o, [x]))

    def FILL(o, v):
        note("v", lambda: g.vector.memset(o[0], v), [o], [], vcost(o, []))

    def ACT(o, x, func=AF.Copy, bias=None, scale=None):
        kw = {}
        if bias is not None: kw["bias"] = bias[0]
        if scale is not None: kw["scale"] = scale[0] if isinstance(scale, tuple) else scale
        note("s", lambda: g.scalar.activation(o[0], x[0], func, **kw), [o],
             [x] + [s for s in (bias, scale) if isinstance(s, tuple)], vcost(o, [x]) + .015)

    def MM(o, pairs, start=True, stop=True):
        def go():
            for i, z in enumerate(pairs):
                k = g.tensor.matmul((z[2] if len(z) > 2 else o)[0], z[0][0], z[1][0], start and i == 0, stop and i == len(pairs) - 1)
            return k
        f = [max(64, z[1][2]) * PE[0] * (4 if SCRATCH[z[0][1][0][0]][2] == "float32" else 1) for z in pairs]
        note("p", go, [o], [y for z in pairs for y in z[:2]], sum(f), lat=.06)

    def DMA(q, o, x, sem):
        note(q, lambda: Q[q].dma_start(o[0], x[0]), [o], [x], .1, sem, 16, 4.0)

    def SUMS(mat, buf, base, n):
        return [(A(mat, jj * 128, jj * 128 + 128), A(buf, base + jj, base + 16 * n, 16)) for jj in range(16)]

    def IOTA(pattern, b, cm, base=0):
        note("g", lambda: g.iota(b[0], pattern, base, cm), [b], [], .13 + 2 * b[2] * CY)

    def H(ap):
        return (ap, [], 0)

    DMA("y", A("wti", 0, 1), H(T.wt[:]), "dw")
    DMA("y", A("xa", 0, P // 2), H(T.x[:, 0:P // 2]), "dx0")
    DMA("s", A("tmo"), H(T.tm[:]), "dt")
    DMA("y", A("xa", P // 2, P), H(T.x[:, P // 2:P]), "dx1")
    DMA("y", A("kmi", 0, 15), H(T.km[:]), "dk")

    IOTA([[0, 1]], A("ipart", 0, 1), 1)
    IOTA([[1, 128]], A("ic"), 0)
    for k in (0, 1):
        IOTA([[-1000, 8], [1, 8], [1000, 16]], A("io2", 1024 * k, 1024 * k + 1024), 0, -8000 * k)
    C = lambda i: A("cf", i, i + 1)
    (JJ, GK, IPF, F15, R15N, FIRST, NF, ODD, MH, SX, ST, CW, CMD, CMF, CMZ, CJ, CK, CB, CTH, CC2, C2047, C8K, CMH2, CQ, CP23, CM23, C1,
     CM2047) = [C(i) for i in range(28)]
    TS(A("ci", 0, 1), A("ipart", 0, 1), 15, OP.bitwise_and)
    TS(A("ci", 1, 2), A("ipart", 0, 1), 4, OP.arith_shift_right)
    TS(A("ci", 2, 3), A("ipart", 0, 1), 1, OP.bitwise_and)
    CP(JJ, A("ci", 0, 1)); CP(GK, A("ci", 1, 2)); CP(ODD, A("ci", 2, 3)); CP(IPF, A("ipart", 0, 1))
    TS(F15, JJ, 15.0, OP.is_lt)
    TS(FIRST, JJ, 0.0, OP.is_equal)
    TS(NF, JJ, 0.0, OP.is_gt)
    CP(CW, A("wti", 0, 1))
    TS(CMD, F15, -8192.0, OP.mult, -8192.0, OP.add)
    TS(CMF, F15, 8192.0, OP.mult)
    TS(CMZ, F15, 2047.0, OP.mult, 1.0, OP.add)
    TS(CJ, F15, 2.0, OP.mult, -1.0, OP.add)
    TS(CK, F15, -2.0, OP.mult)
    TS(R15N, F15, 1.0, OP.mult, -1.0, OP.add)
    TS(CB, R15N, -1.0, OP.mult)
    TS(MH, F15, 0.5, OP.mult)
    TS(CMH2, MH, -1.0, OP.mult, 1.0, OP.add)
    TS(SX, JJ, float(SPX), OP.add, NF, OP.mult)
    TS(ST, JJ, float(TW), OP.add, NF, OP.mult)
    for b, v in ((CTH, -8192.0 * (SELF_D - 7)), (CC2, 1024.0 * SELF_D), (C2047, 2047.0), (C8K, 8192.0), (CQ, -0.25),
                 (CP23, 8388608.0), (CM23, -8388608.0), (C1, 1.0), (CM2047, -2047.0)):
        FILL(b, v)
    TS(A("idn"), A("ic"), IPF, OP.is_equal)
    TS(A("tmpi"), A("ic"), 4, OP.arith_shift_right)
    TS(A("grp"), A("tmpi"), GK, OP.is_equal)
    TS(A("tmpj"), A("ic"), 15, OP.bitwise_and)
    TS(A("emn"), A("tmpj"), 15.0, OP.is_equal, F15, OP.mult)
    TT(A("prd"), A("emn"), A("grp"), OP.mult)
    TS(A("idf"), A("idn"), F15, OP.mult)
    TT(A("em"), A("idf"), A("prd"), OP.subtract)
    for k in (0, 1):
        TS(A("wb", 1024 * k, 1024 * k + 1024), A("io2", 1024 * k, 1024 * k + 1024), GK, OP.is_equal, CW, OP.mult)
    TS(A("md"), A("io2"), GK, OP.is_equal, CMD, OP.mult)
    TS(A("bm"), A("io2"), GK, OP.is_equal)
    ACT(A("mf"), A("bm"), AF.Copy, None, CMF)
    ACT(A("mz"), A("bm"), AF.Copy, None, CMZ)
    CP(A("kmf", 0, 15), A("kmi", 0, 15))
    TS(A("nt"), A("ic"), 16.0, OP.mult, JJ, OP.add)
    TS(A("nt8"), A("nt"), 8.0, OP.mult, -8192.0, OP.add)
    TS(A("ntm"), A("nt"), -2047.0, OP.add)
    PL = A("ps0", 0, 128)
    CP(PL, A("nt"))
    TS(A("idj"), A("idn"), CJ, OP.mult)
    TS(A("idk"), A("idn"), CK, OP.mult)
    TS(A("ids"), A("idn"), float(SELF_D * 8192), OP.mult)
    TS(A("idc"), A("idn"), float(SELF_D * 1024), OP.mult)
    TS(A("id1"), A("idn"), 2048.0, OP.mult)
    TS(A("id2"), A("idn"), 4096.0, OP.mult)
    TS(A("idm"), A("idn"), -1.0, OP.mult)
    TS(A("id16"), A("ic"), IPF, OP.is_equal)
    TS(A("idnf"), A("ic"), IPF, OP.is_equal)
    TS(A("m16"), A("ic", 0, 16), JJ, OP.is_equal)
    FILL(A("one"), 1.0); FILL(A("nd"), 0.0); FILL(A("upd"), 0.0)

    sent, arrived = [0], {}

    def send_table(o):
        d = cores[(rank - o) % NR]
        rid, pid = topo.addr(d, core)
        sent[0] += len(topo.engines(core, d))
        arrived["tma%d" % o] = len(topo.engines(cores[(rank + o) % NR], core))
        k = note("g", lambda: g.remote_dma(T["tb%d" % o][:, 0:TW], T.tmo[:], T.sem["tma%d" % o], T.sem.ls, pid, rid, topo.mask(core, d)),
                 [], [A("tmo")], .5, None)
        note("x", None, [A("tb%d" % o, 0, TW)], [], 0, None, 1, 4.0 + 6 * o, ("tma%d" % o, arrived["tma%d" % o]), (k,))
    for o in (1, 2, 3): send_table(o)

    cc = lambda i: A("c", i, i + 1)
    ii = lambda i: A("cii", i, i + 1)
    seen, landed = set(), {}

    def updates(t):
        o = 1 + t % 3
        for t0 in range(t):
            if (t0, o) in landed and (t0, o) not in seen:
                seen.add((t0, o))
                k = landed[(t0, o)]
                L = A("l1", 4 + 2 * (len(seen) % 2), 5 + 2 * (len(seen) % 2))
                TS(L, A("land", 16 * k + 1, 16 * k + 2), FIRST, OP.mult, ST, OP.add)
                CP(IND(A("tb%d" % o), L), A("land", 16 * k, 16 * k + 16))

    def shares(r, t):
        src, dst = cores[r], {o: cores[(r - o) % NR] for o in SENDS[t]}
        away = [o for o in SENDS[t] if dst[o] not in topo.cores_of(src)]
        off = topo.engines(src, dst[away[0]])
        w = len(off) // len(away)
        es = {o: off[i * w:i * w + w] for i, o in enumerate(away)}
        for o in SENDS[t]:
            if o not in es: es[o] = [e for e in topo.engines(src, dst[o]) if e not in off]
        return es

    def send_new(t):
        es, xs = shares(rank, t), []
        for o in SENDS[t]:
            rid, pid = topo.addr(cores[(rank - o) % NR], core)
            k = len(landed)
            landed[(t, o)] = k
            xs.append(RemoteDMATransfer(dst_ids=[DstId(rid=rid, pnc=pid)], dma_engine_mask=sum(1 << e for e in es[o]),
                                        remote_sem=T.sem["ua%d_%d" % (t, o)], src=T.upd[:, 16 * t:16 * t + 16],
                                        dst=T.land[:, 16 * k:16 * k + 16]))
            sent[0] += len(es[o])
            arrived["ua%d_%d" % (t, o)] = len(shares((rank + o) % NR, t)[o])
        me = note("g", lambda: g.remote_dma_fused(xs, local_sem=T.sem.ls), [], [A("upd", 16 * t, 16 * t + 16)], .5, None)
        for o in SENDS[t]:
            k, s = landed[(t, o)], "ua%d_%d" % (t, o)
            note("x", None, [A("land", 16 * k, 16 * k + 16)], [], 0, None, 1, LATE, (s, arrived[s]), (me,))

    def one_round(t):
        X, XN = ("xa", "xb") if t % 2 == 0 else ("xb", "xa")
        TB = "tb%d" % (1 + t % 3)
        MM(A("ps1", 0, 128), SUMS("wb", X, 0, NC))
        for k in range(4):
            b = A(["z2", "z0", "z1", "ps2"][k])
            MM(b, [(A("em"), A(X, 512 * k, 512 * k + 512))])
            ACT(A("xf", 512 * k, 512 * k + 512), b, AF.Identity, R15N)
        for k in range(4):
            ACT(A(X, P + 512 * k, P + 512 * k + 512), A(X, 512 * k, 512 * k + 512), AF.Identity, CB, CJ)
        MM(A("ps5", 0, 128), SUMS("mf", X, 0, NC))
        CP(A("ui"), A("ps1", 0, 128))
        TS(A("u"), A("ui"), 4095, OP.bitwise_and)
        TT(A("sq"), A("u"), A("u"), OP.mult)
        TS(A("s5"), A("sq"), 5, OP.arith_shift_right)
        for m in range(M):
            a, b = 128 * m, 128 * m + 128
            TS(A("ps0", a + 128, b + 128), A("u"), A("kmf", 3 * t + m, 3 * t + m + 1), OP.mult)
            TT(A("t3", a, b), A("s5"), A("ps0", a + 128, b + 128), OP.add)
            TS(A("q3", a, b), A("t3", a, b), P - 1, OP.bitwise_and)
            CP(A("l3", a, b), A("q3", a, b))
            TT(A("eqb", a, b), A("q3", a, b), PL, OP.is_equal)
            CP(A("q16", a, b), A("q3", a, b))
        ACT(A("nf"), A("ps5", 0, 128), AF.Identity, C8K, -1.0)
        TT(A("pt"), A("nt8"), A("ps5", 0, 128), OP.add)

        def pick(out, tab, lst, a, b, i):
            for k, h in enumerate(range(a, b, 32)):
                o, x = A(out, 16 * h, 16 * min(h + 32, b)), IND(A(tab, 0, P), A(lst, h, min(h + 32, b)))
                if i in SPL and k % 2: CP(o, x)
                else: ACT(o, x, AF.Copy)

        def near(c, i):
            c0, n = c
            a = 16 * c0
            e = lambda m: A("eqb", 128 * m + c0, 128 * m + c0 + n)
            k = lambda m: A("q16", 128 * m + c0, 128 * m + c0 + n)
            l = lambda m: A("l3", 128 * m + c0, 128 * m + c0 + n)
            o0, o1 = A("ps2", 0, n), A("ps2", n, 2 * n)
            for m in range(2 if i in SM else 3):
                TT(A("mn", 3 * a + 16 * n * m, 3 * a + 16 * n * (m + 1)), IND(A("xf"), l(m)), A(X, a, a + 16 * n), OP.min)
            MM(A("ps2", 0, 2 * n), SUMS("md", "mn", 48 * c0, 2 * n) +
               [(A("ids"), e(0), o0), (A("ids"), e(1), o1), (A("id1"), A("one", 0, n), o1), (A("id16"), k(0), o0), (A("id16"), k(1), o1)])
            last = [(A("ids"), e(2)), (A("id2"), A("one", 0, n)), (A("id16"), k(2))]
            if i in SM:
                for p0 in range(a, a + 16 * n, 512):
                    p1 = min(p0 + 512, a + 16 * n)
                    w = A("z2", 0, p1 - p0)
                    ACT(A("xs", p0, p1), IND(A(X, 0, P), A("l3", 256 + p0 // 16, 256 + p1 // 16)), AF.Copy)
                    MM(w, [(A("idm"), A(X, p0, p1)), (A("idn"), A("xs", p0, p1))])
                    ACT(A("as", p0, p1), w, AF.Abs)
                MM(A("ps3", 0, n), SUMS("mf", "as", a, n) + last + [(A("idnf"), A("nf", c0, c0 + n))])
            else:
                MM(A("ps3", 0, n), SUMS("md", "mn", 48 * c0 + 32 * n, n) + last)
            ACT(A("v3", c0, c0 + n), o0, AF.Copy)
            TT(A("vmn", c0, c0 + n), A("v3", c0, c0 + n), o1, OP.min)

        def choose(c, i):
            a, b, n = c[0], c[0] + c[1], c[1]
            TT(A("vm", a, b), A("vmn", a, b), A("ps3", 0, n), OP.min)
            TS(A("qs", a, b), A("vm", a, b), P - 1, OP.bitwise_and)
            CP(A("lq", a, b), A("qs", a, b))
            pick("xq", X, "lq", a, b, i)
            MM(A("ps5", 128, 128 + n), SUMS("wb", "xq", 16 * a, n))
            TS(A("b1", a, b), A("vm", a, b), -8192, OP.bitwise_and)
            TT(A("b4", a, b), A("b1", a, b), A("pt", a, b), OP.add)
            ACT(A("sg", a, b), A("b4", a, b), AF.Sign, CTH)
            ACT(A("bq", a, b), A("b4", a, b), AF.Identity, CC2, 0.25)
            TT(A("lo", a, b), A("qs", a, b), A("ps0", a, b), OP.min)

        def asked(c, i):
            a, b, n = c[0], c[0] + c[1], c[1]
            CP(A("ri", a, b), A("ps5", 128, 128 + n))
            TS(A("uq", a, b), A("ri", a, b), 4095, OP.bitwise_and)
            TT(A("hp", a, b), A("uq", a, b), A("u", a, b), OP.mult)
            TS(A("hs", a, b), A("hp", a, b), 4, OP.arith_shift_right, TW - 1, OP.bitwise_and)
            CP(A("lh", a, b), A("hs", a, b))
            sg = [(A("z%d" % (k % 2), 0, min(512, 16 * b - p0)), p0, min(p0 + 512, 16 * b)) for k, p0 in enumerate(range(16 * a, 16 * b, 512))]
            for z, p0, p1 in sg:
                MM(z, [(A("idj"), A(X, p0, p1)), (A("idn"), A("xq", p0, p1))], True, False)
            pick("ag", TB, "lh", a, b, i)
            for z, p0, p1 in sg:
                MM(z, [(A("idk"), A("ag", p0, p1))], False, True)
                ACT(A("az", p0, p1), z, AF.Abs)

        def keyed(c):
            a, b = c[0], c[0] + c[1]
            MM(A("ps1", a, b), SUMS("mz", "az", 16 * a, c[1]) + [(A("idc"), A("sg", a, b))])
            TT(A("key", a, b), A("bq", a, b), A("ps1", a, b), OP.add)

        AC, BC, INV, NIN, BA, B1, B1I, RD, SL, BS, AB, RI = [cc(i) for i in range(10, 22)]
        E0, E1, E2 = [A("ps0", 128 * m + 128, 128 * m + 256) for m in range(3)]
        updates(t)
        for i, c in enumerate(CH):
            bon[0] = BON * (len(CH) - i)
            near(c, i)
            choose(c, i)
            asked(c, i)
        for i, c in enumerate(CH):
            bon[0] = BON * (len(CH) - i)
            keyed(c)
            a, b = c[0], c[0] + c[1]
            e = A("ps0", 128 + a, 128 + b)
            CP(A("ki", a, b), A("key", a, b))
            TS(A("kv", a, b), A("ki", a, b), 1, OP.bitwise_and)
            TS(e, A("kv", a, b), -4096.0, OP.mult)
            TT(A("lod", a, b), A("lo", a, b), e, OP.add)
        bon[0] = 0.0

        def lowest(src, out, dg):
            RED(out, src, OP.min)
            TS(A(dg), A("m16"), out, OP.mult)
            MM(A("ps1", 0, 16), [(A("grp"), A(dg))])

        lowest(A("key"), cc(0), "dg")
        RED(cc(1), A("ps1", 0, 16), OP.min)
        TS(E1, A("key"), cc(1), OP.is_equal)
        TT(A("prd"), A("qs"), E1, OP.mult)
        RED(cc(2), A("prd"), OP.add)
        MM(A("ps1", 0, 1), [(A("grp"), cc(2))])
        if t < RO - 1:
            TT(A("prh"), A("hs"), E1, OP.mult)
            RED(cc(27), A("prh"), OP.add)
            MM(A("ps3", 64, 65), [(A("grp"), cc(27))])
            CP(A("upd", 16 * t + 1, 16 * t + 2), A("ps3", 64, 65))
        CP(ii(0), cc(1))
        TS(ii(1), ii(0), 1, OP.arith_shift_right, P - 1, OP.bitwise_and)
        TS(ii(2), ii(0), 1, OP.bitwise_and)
        CP(INV, ii(2))
        ACT(NIN, INV, AF.Identity, C1, -1.0)
        TT(AC, ii(1), A("ps1", 0, 1), OP.min)
        TT(BC, ii(1), A("ps1", 0, 1), OP.max)
        TS(E0, A("lod"), AC, OP.is_le, BIG, OP.mult)
        TT(A("k2a"), A("key"), E0, OP.max)
        TS(E2, A("lod"), BC, OP.is_ge, BIG, OP.mult)
        TT(A("k2"), A("k2a"), E2, OP.max)
        lowest(A("k2"), cc(3), "dg2")
        RED(cc(4), A("ps1", 0, 16), OP.min)
        TS(E0, A("k2"), cc(4), OP.is_equal)
        TT(A("prk"), A("qs"), E0, OP.mult)
        RED(cc(5), A("prk"), OP.add)
        MM(A("ps1", 0, 1), [(A("grp"), cc(5))])
        CP(ii(4), cc(4))
        TS(ii(5), ii(4), 1, OP.arith_shift_right, P - 1, OP.bitwise_and)
        TS(cc(6), cc(4), BIG, OP.is_lt, NIN, OP.mult)
        ACT(BA, AC, AF.Identity, BC, -1.0)
        ACT(RD, BA, AF.Copy, None, NIN)
        ACT(RI, INV, AF.Identity, RD, float(P + 1))
        ACT(AB, AC, AF.Identity, BC)
        ACT(BS, AB, AF.Identity, RI, INV)
        ACT(SL, INV, AF.Copy, None, -2.0)
        ACT(A("rn"), A("nt"), AF.Identity, BS, SL)
        ACT(A("nb2"), A("ntm"), AF.Identity, BA)
        ACT(B1, BC, AF.Identity, C2047, -1.0)
        ACT(B1I, B1, AF.Copy, None, NIN)
        ACT(cc(32), BC, AF.Identity, CM2047)
        TS(A("l1", 0, 1), ODD, BA, OP.mult, AC, OP.add)
        ACT(A("nc"), IND(A(X, 0, P), A("l1", 0, 1)), AF.Copy)
        TS(A("l1", 2, 3), FIRST, AC, OP.mult, SX, OP.add)
        ACT(cc(22), A("nc", 0, 1), AF.Identity, CQ, CMH2)
        ACT(cc(28), A("nc", 1, 2), AF.Identity, cc(22), MH)
        ACT(cc(29), cc(28), AF.Identity, CP23)
        ACT(A("nd", 0, 1), cc(29), AF.Identity, CM23)
        CP(IND(A(X), A("l1", 2, 3)), A("nd"))
        if t < RO - 1:
            ACT(A("upd", 16 * t, 16 * t + 1), A("nd", 0, 1), AF.Copy)
            send_new(t)
        ACT(cc(30), AC, AF.Copy, None, -1.0)
        ACT(cc(31), BC, AF.Copy, None, -1.0)
        ACT(A("ma"), A("nt"), AF.Sign, cc(30))
        ACT(A("mb"), A("nt"), AF.Sign, cc(31))
        ACT(A("ma"), A("ma"), AF.Relu)
        ACT(A("mb"), A("mb"), AF.Relu, None, INV)
        MM(A("z0", 0, 128), [(A("idn"), A("ma")), (A("idm"), A("mb"))])
        TT(E2, A("rn"), A("z0", 0, 128), OP.mult)
        TT(A("bs"), A("nt"), E2, OP.add)
        TT(cc(8), ii(5), A("ps1", 0, 1), OP.max)
        TT(cc(7), ii(5), A("ps1", 0, 1), OP.min)
        TS(cc(9), cc(8), BC, OP.is_gt, cc(6), OP.mult)
        TT(cc(23), cc(8), cc(7), OP.subtract)
        TS(cc(25), cc(23), cc(32), OP.add, cc(9), OP.mult)
        TS(cc(24), cc(8), 2047.0, OP.subtract, cc(9), OP.mult)
        TT(cc(26), cc(25), B1I, OP.add)
        TS(E0, A("nb2"), cc(25), OP.is_gt, RD, OP.mult)
        TT(A("y1"), A("bs"), E0, OP.subtract)
        TS(E2, A("ntm"), cc(24), OP.is_gt, cc(26), OP.mult)
        TS(A("g2"), A("nb2"), cc(24), OP.is_gt, cc(26), OP.mult)
        TT(E2, A("g2"), E2, OP.subtract)
        TT(A("sf"), A("y1"), E2, OP.subtract)
        CP(A("ls"), A("sf"))
        Y = "yb" if t == RO - 1 else XN
        for k in (0, 1):
            CP(A(Y, 512 * k, 512 * k + 512), IND(A(X, 0, 2 * P), A("ls", 32 * k, 32 * k + 32)))
            ACT(A(Y, 1024 + 512 * k, 1536 + 512 * k), IND(A(X, 0, 2 * P), A("ls", 64 + 32 * k, 96 + 32 * k)), AF.Copy)
        if t == RO - 1:
            for k in range(4):
                DMA("ysys"[k], H(T.y[:, 512 * k:512 * k + 512]), A("yb", 512 * k, 512 * k + 512), "dy%d" % k)

    for t in range(RO):
        one_round(t)

    n = len(ops)
    post, left, tail = [[] for _ in ops], [len(o["pre"]) for o in ops], [0.0] * n
    for i in range(n - 1, -1, -1):
        o = ops[i]
        for j in o["pre"]: post[j].append(i)
        tail[i] = o["cost"] + o["lat"] + WAKE + max([tail[j] for j in post[i]] + [0.0])
    pri = list(tail)
    for i in range(n - 1, -1, -1): pri[i] = max([tail[i] + ops[i]["bon"]] + [pri[j] + ops[i]["cost"] for j in post[i]])
    ready, free, at, order = {}, {}, [0.0] * n, []
    for i in range(n):
        if not left[i]: ready.setdefault(ops[i]["q"], []).append(i)
    while len(order) < n:
        best = None
        for q in sorted(ready):
            if ready[q]:
                st = lambda i: at[i] if q == "x" else max(at[i], free.get(q, 0.0))
                s0 = min(st(i) for i in ready[q])
                i = max([i for i in ready[q] if st(i) <= s0 + .05], key=lambda i: (pri[i], -i))
                if best is None or st(i) < best[0]: best = (st(i), q, i)
        s0, q, i = best
        ready[q].remove(i)
        order.append(i)
        free[q] = s0 + ops[i]["cost"]
        for j in post[i]:
            at[j] = max(at[j], free[q] + ops[i]["lat"] + WAKE)
            left[j] -= 1
            if not left[j]: ready.setdefault(ops[j]["q"], []).append(j)

    clk, total, evs = {q: {} for q in list(Q) + ["x"]}, dict(arrived), {}
    for i in order:
        o, q, need = ops[i], ops[i]["q"], {}
        if q == "x":
            evs[i] = (o["ev"], {})
            continue
        for j in o["pre"]:
            if evs[j] is not None:
                (s, v), snap = evs[j]
                if clk[q].get(s, 0) < v and need.get(s, (0,))[0] < v: need[s] = (v, snap)
        items = sorted(need.items())
        for s, (v, snap) in items:
            if not any(s2 != s and sn2.get(s, 0) >= v for s2, (v2, sn2) in items): Q[q].wait_ge(T.sem[s], v)
        for s, (v, snap) in items:
            for s2, v2 in list(snap.items()) + [(s, v)]: clk[q][s2] = max(clk[q].get(s2, 0), v2)
        call = o["fn"]()
        if o["sem"] is None:
            evs[i] = None
            continue
        s = o["sem"] or QS[q]
        call.then_inc(T.sem[s], o["inc"])
        total[s] = total.get(s, 0) + o["inc"]
        evs[i] = ((s, total[s]), dict(clk[q]))
    total["ls"] = sent[0]
    for s in sorted(total):
        g.wait_ge(T.sem[s], total[s])
